import numpy as np
import ml_dtypes


def mxq(x, axis, fmt="e4m3"):
    dtype, down = {"e4m3": (ml_dtypes.float8_e4m3fn, 7), "e5m2": (ml_dtypes.float8_e5m2, 14)}[fmt]
    v = np.moveaxis(np.asarray(x, np.float32).astype(ml_dtypes.bfloat16).astype(np.float64), axis, -1)
    blocks = v.reshape(v.shape[:-1] + (-1, 32))
    amax = np.abs(blocks).max(-1, keepdims=True)
    byte = np.maximum(np.where(amax > 0, np.frexp(amax)[1] - 1 + 127, 0) - down, 1)
    scale = np.exp2(byte - 127.0)
    codes = (blocks / scale).astype(np.float32).astype(dtype).astype(np.float64)
    return np.moveaxis((codes * scale).reshape(v.shape), -1, axis)


WIDE = False


def mx_kscale(k):
    if not WIDE:
        return np.ones(k)
    levels = np.array([10, -10, 5, -5, 0])
    if k % 512:
        return np.exp2(np.random.permutation(np.resize(levels, k // 32))).repeat(32)
    a = np.empty((k // 512, 16))
    for p in range(k // 512):
        a[p, :8] = np.random.permutation(np.resize(levels, 8))
        for g in range(8):
            far = levels[np.abs(levels - a[p, g]) >= 10]
            a[p, g + 8] = far[np.random.randint(len(far))]
    return np.exp2(a.ravel()).repeat(32)


def f64(x):
    return np.asarray(x).astype(np.float64)


def striped(idx):
    return np.tile(np.asarray(idx).reshape(-1, 16).T, (8, 1)).astype(np.uint16)


def unstriped(offs):
    return offs[:16].T.reshape(-1).astype(np.int64)


E2M1 = np.array([0.0, 0.5, 1.0, 1.5, 2.0, 3.0, 4.0, 6.0, -0.0, -0.5, -1.0, -1.5, -2.0, -3.0, -4.0, -6.0])


def pack_weight(w, fmt):
    k, n = w.shape
    w = f64(np.asarray(w, np.float32).astype(ml_dtypes.bfloat16)).reshape(k // 32, 32, n)
    amax = np.abs(w).max(1)
    if fmt == "e4m3":
        byte = np.frexp(amax)[1] - 1 + 127 - 7
    else:
        mant, ex = np.frexp(amax / 6.0)
        byte = np.where(mant > 0.5, ex, ex - 1) + 127
    byte = np.clip(np.where(amax > 0, byte, 1), 1, 254)
    scaled = (w * np.exp2(127.0 - byte)[:, None, :]).reshape(k, n).astype(np.float32)
    by_word = np.ascontiguousarray(scaled.reshape(k // 512, 128, 4, n).transpose(0, 1, 3, 2))
    if fmt == "e4m3":
        words = by_word.astype(ml_dtypes.float8_e4m3fn).view(np.uint8)
    else:
        c = by_word.astype(ml_dtypes.float4_e2m1fn).view(np.uint8) & 0xF
        words = (c[..., 0::2] | (c[..., 1::2] << 4)).reshape(k // 512, 128, 2 * n)
    return np.ascontiguousarray(words), np.ascontiguousarray(byte.astype(np.uint8).reshape(k // 512, 16, n))


def unpack_weight(words, scales, fmt):
    g, _, n = scales.shape
    words = np.ascontiguousarray(words).reshape(g, 128, n, -1)
    if fmt == "e4m3":
        vals = words.view(ml_dtypes.float8_e4m3fn).astype(np.float64)
    else:
        nib = np.empty((g, 128, n, 4), np.uint8)
        nib[..., 0::2] = words & 0xF
        nib[..., 1::2] = words >> 4
        vals = E2M1[nib]
    vals = vals * np.repeat(np.exp2(scales.astype(np.float64) - 127.0), 8, axis=1)[..., None]
    return vals.transpose(0, 1, 3, 2).reshape(g * 512, n)


B, N, T, D, NQ = 1, 512, 2048, 512, 256


def setup_inputs():
    n = np.random.standard_normal
    idx = np.random.permutation(T)[:B * N]
    s = mx_kscale(D)[:, None]
    kp = pack_weight(n((D, T)) / s, "e4m3")
    return {
        "qT": (n((B, D, NQ)) * s * (1.00 / np.sqrt(D))).astype(np.float32),
        "k_words": kp[0],
        "k_scales": kp[1],
        "kb": np.tile(n(2048), (128, 1)).astype(np.float32),
        "rt": (n((B, NQ, N))).astype(np.float32),
        "ub": (0.5 * n((B, NQ, 1))).astype(np.float32),
        "wt": (np.random.uniform(0.1, 1.0, (B, NQ, N))).astype(np.float32),
        "offs": striped(idx),
    }


def reference(qT, k_words, k_scales, kb, rt, ub, wt, offs):
    idx = unstriped(offs)
    pick = lambda x, which: x[:, which].reshape(x.shape[0], B, -1).transpose(1, 0, 2)
    k = unpack_weight(k_words, k_scales, "e4m3")
    kg = pick(k, idx)
    qq = mxq(f64(qT), 1, "e4m3")
    a = qq.transpose(0, 2, 1) @ kg
    y = (f64(rt) - a - pick(f64(kb), idx)[:, :1, :] - f64(ub)) * f64(wt)
    return y

@@ -1,0 +1,115 @@
+from contextlib import ExitStack
+
+import concourse.mybir as mybir
+from concourse.masks import make_identity
+
+F32 = mybir.dt.float32
+BF16 = mybir.dt.bfloat16
+I32 = mybir.dt.int32
+U32 = mybir.dt.uint32
+U16 = mybir.dt.uint16
+U8 = mybir.dt.uint8
+FP8X4 = mybir.dt.float8_e4m3fn_x4
+SUB = mybir.AluOpType.subtract
+MULT = mybir.AluOpType.mult
+
+P = 128
+PACK = 4
+D = 512
+NQ = 256
+N = 512
+T = 2048
+QT = NQ // P
+QUAD = 32
+CH = N // P
+
+FLOPS = 2 * D * NQ * N
+BYTES = 4 * D * NQ + D * T + (D // 32) * T + 4 * T + 3 * 4 * NQ * N + 4 * NQ + 2 * P * (N // 16)
+
+
+def tile_attend_link_resid_topk_kernel(tc, qT, k_words, k_scales, kb, rt, ub, wt, offs, out):
+    nc = tc.nc
+    with ExitStack() as ctx:
+        keep = ctx.enter_context(tc.tile_pool(name="keep", bufs=1))
+        psum = ctx.enter_context(tc.psum_pool(name="psum", bufs=1))
+
+        offsets = keep.tile([P, N // 16], U16, name="offsets")
+        nc.sync.dma_start(offsets[:], offs)
+
+        q_raw = keep.tile([P, PACK, NQ], F32, name="q_raw", tag="stage")
+        nc.scalar.dma_start(out=q_raw[:], in_=qT[0].rearrange("(p j) w -> p j w", j=PACK))
+        word_pool = keep.tile([P, T], I32, name="word_pool")
+        nc.scalar.dma_start(out=word_pool[:], in_=k_words[0].rearrange("p n r -> p (n r)").bitcast(I32))
+        rt_sb = keep.tile([P, QT, N], F32, name="rt_sb")
+        nc.scalar.dma_start(out=rt_sb[:], in_=rt[0].rearrange("(p t) n -> p t n", t=QT))
+
+        scale_pool = keep.tile([P, T], U8, name="scale_pool")
+        nc.vector.memset(scale_pool[:].bitcast(I32), 0)
+        for quad in range(P // QUAD):
+            nc.sync.dma_start(
+                out=scale_pool[QUAD * quad : QUAD * quad + PACK, :].bitcast(I32),
+                in_=k_scales[0, PACK * quad : PACK * (quad + 1), :].bitcast(I32),
+            )
+        kb_pool = keep.tile([P, T], F32, name="kb_pool", tag="reused", align_bytes=64)
+        nc.vector.memset(kb_pool[:], 0.0)
+        nc.sync.dma_start(out=kb_pool[0:1, :], in_=kb[0:1, :])
+
+        ident = keep.tile([P, P], F32, name="ident")
+        make_identity(nc, ident[:])
+        ub_sb = keep.tile([P, QT], F32, name="ub_sb")
+        nc.gpsimd.dma_start(out=ub_sb[:], in_=ub[0].rearrange("(p t) o -> p (t o)", t=QT))
+        warm = keep.tile([P, 1], F32, name="warm")
+        nc.scalar.copy(out=warm[:], in_=ident[:, 0:1])
+
+        k_scale = keep.tile([P, N], U8, name="k_scale", align_bytes=64)
+        nc.vector.tensor_copy(k_scale[:], scale_pool[:].indirect(offsets[:]))
+        kb_row = keep.tile([P, N], F32, name="kb_row")
+        nc.vector.tensor_copy(kb_row[:], kb_pool[:].indirect(offsets[:]))
+
+        q_bf = keep.tile([P, QT, P, PACK], BF16, name="q_bf", align_bytes=64)
+        nc.scalar.copy(out=q_bf[:], in_=q_raw[:].rearrange("p j (m t) -> p t m j", t=QT))
+        wt_sb = keep.tile([P, QT, N], F32, name="wt_sb", tag="stage")
+        nc.scalar.dma_start(out=wt_sb[:], in_=wt[0].rearrange("(p t) n -> p t n", t=QT))
+
+        turned = psum.tile([P, CH, P], F32, name="turned")
+        for c in range(CH):
+            nc.tensor.transpose(turned[:, c, :], kb_row[:, c * P : (c + 1) * P], ident[:])
+        kb_col = keep.tile([P, CH], F32, name="kb_col")
+        nc.scalar.copy(out=kb_col[:], in_=turned[:, :, 0])
+        kb_all = psum.tile([P, N], F32, name="kb_all")
+        for c in range(CH):
+            nc.tensor.transpose(kb_all[:, c * P : (c + 1) * P], kb_col[:, c : c + 1].to_broadcast([P, P]), ident[:])
+
+        q_code = keep.tile([P, NQ], U32, name="q_code", align_bytes=64)
+        q_scale = keep.tile([P, NQ], U8, name="q_scale", align_bytes=64)
+        nc.vector.quantize_mx(
+            out=q_code[:].bitcast(FP8X4), scales=q_scale[:], in_=q_bf[:].rearrange("p t m j -> p (t m j)")
+        )
+
+        k_code = keep.tile([P, N], U32, name="k_code", tag="reused", align_bytes=64)
+        nc.vector.tensor_copy(k_code[:], word_pool[:].bitcast(U32).indirect(offsets[:]))
+
+        out_v = out[0].rearrange("(p t) n -> p t n", t=QT)
+        acc = [psum.tile([P, N], F32, name=f"acc{t}") for t in range(QT)]
+        unbiased = [keep.tile([P, N], F32, name=f"unbiased{t}") for t in range(QT)]
+        resid = [keep.tile([P, N], F32, name=f"resid{t}") for t in range(QT)]
+        res = [keep.tile([P, N], F32, name=f"res{t}") for t in range(QT)]
+        for t in range(QT):
+            nc.tensor.matmul_mx(
+                out=acc[t][:],
+                lhsT=q_code[:, t * P : (t + 1) * P].bitcast(FP8X4),
+                lhsT_scale=q_scale[:, t * P : (t + 1) * P],
+                rhs=k_code[:].bitcast(FP8X4),
+                rhs_scale=k_scale[:],
+                start=True,
+                stop=True,
+            )
+        for t in range(QT):
+            nc.vector.scalar_tensor_tensor(
+                out=unbiased[t][:], in0=rt_sb[:, t, :], scalar=ub_sb[:, t : t + 1], in1=kb_all[:], op0=SUB, op1=SUB
+            )
+        for t in range(QT):
+            nc.vector.tensor_tensor(out=resid[t][:], in0=unbiased[t][:], in1=acc[t][:], op=SUB)
+        for t in range(QT):
+            nc.vector.tensor_tensor(out=res[t][:], in0=resid[t][:], in1=wt_sb[:, t, :], op=MULT)
+            nc.sync.dma_start(out=out_v[:, t, :], in_=res[t][:])

@@ -36,39 +36,41 @@ def tile_attend_link_resid_topk_kernel(tc, qT, k_words, k_scales, kb, rt, ub, wt
         offsets = keep.tile([P, N // 16], U16, name="offsets")
         nc.sync.dma_start(offsets[:], offs)
 
-        q_raw = keep.tile([P, PACK, NQ], F32, name="q_raw", tag="stage")
-        nc.scalar.dma_start(out=q_raw[:], in_=qT[0].rearrange("(p j) w -> p j w", j=PACK))
-        word_pool = keep.tile([P, T], I32, name="word_pool")
-        nc.scalar.dma_start(out=word_pool[:], in_=k_words[0].rearrange("p n r -> p (n r)").bitcast(I32))
-        rt_sb = keep.tile([P, QT, N], F32, name="rt_sb")
-        nc.scalar.dma_start(out=rt_sb[:], in_=rt[0].rearrange("(p t) n -> p t n", t=QT))
+        q_raw = keep.tile([P, PACK, NQ], F32, name="q_raw", tag="slot_q")
+        nc.sync.dma_start(out=q_raw[:], in_=qT[0].rearrange("(p j) w -> p j w", j=PACK))
 
-        scale_pool = keep.tile([P, T], U8, name="scale_pool")
+        warm_in = keep.tile([P, 1], F32, name="warm_in", tag="slot_words")
+        nc.vector.memset(warm_in[:], 0.0)
+        warm_out = keep.tile([P, 1], F32, name="warm_out", tag="slot_rt")
+        nc.scalar.copy(out=warm_out[:], in_=warm_in[:])
+
+        kb_pool = keep.tile([P, T], F32, name="kb_pool", tag="slot_kb", align_bytes=64)
+        nc.vector.memset(kb_pool[:], 0.0)
+        nc.sync.dma_start(out=kb_pool[0:1, :], in_=kb[0:1, :])
+        scale_pool = keep.tile([P, T], U8, name="scale_pool", tag="slot_scales", align_bytes=64)
         nc.vector.memset(scale_pool[:].bitcast(I32), 0)
         for quad in range(P // QUAD):
             nc.sync.dma_start(
                 out=scale_pool[QUAD * quad : QUAD * quad + PACK, :].bitcast(I32),
                 in_=k_scales[0, PACK * quad : PACK * (quad + 1), :].bitcast(I32),
             )
-        kb_pool = keep.tile([P, T], F32, name="kb_pool", tag="reused", align_bytes=64)
-        nc.vector.memset(kb_pool[:], 0.0)
-        nc.sync.dma_start(out=kb_pool[0:1, :], in_=kb[0:1, :])
+
+        word_pool = keep.tile([P, T], I32, name="word_pool", tag="slot_words")
+        nc.scalar.dma_start(out=word_pool[:], in_=k_words[0].rearrange("p n r -> p (n r)").bitcast(I32))
+        rt_sb = keep.tile([P, QT, N], F32, name="rt_sb", tag="slot_rt")
+        nc.scalar.dma_start(out=rt_sb[:], in_=rt[0].rearrange("(p t) n -> p t n", t=QT))
 
         ident = keep.tile([P, P], F32, name="ident")
         make_identity(nc, ident[:])
-        ub_sb = keep.tile([P, QT], F32, name="ub_sb")
-        nc.gpsimd.dma_start(out=ub_sb[:], in_=ub[0].rearrange("(p t) o -> p (t o)", t=QT))
-        warm = keep.tile([P, 1], F32, name="warm")
-        nc.scalar.copy(out=warm[:], in_=ident[:, 0:1])
 
-        k_scale = keep.tile([P, N], U8, name="k_scale", align_bytes=64)
-        nc.vector.tensor_copy(k_scale[:], scale_pool[:].indirect(offsets[:]))
         kb_row = keep.tile([P, N], F32, name="kb_row")
         nc.vector.tensor_copy(kb_row[:], kb_pool[:].indirect(offsets[:]))
+        k_scale = keep.tile([P, N], U8, name="k_scale", tag="slot_kb", align_bytes=64)
+        nc.vector.tensor_copy(k_scale[:], scale_pool[:].indirect(offsets[:]))
 
-        q_bf = keep.tile([P, QT, P, PACK], BF16, name="q_bf", align_bytes=64)
+        q_bf = keep.tile([P, QT, P, PACK], BF16, name="q_bf", tag="slot_qbf", align_bytes=64)
         nc.scalar.copy(out=q_bf[:], in_=q_raw[:].rearrange("p j (m t) -> p t m j", t=QT))
-        wt_sb = keep.tile([P, QT, N], F32, name="wt_sb", tag="stage")
+        wt_sb = keep.tile([P, QT, N], F32, name="wt_sb", tag="slot_q")
         nc.scalar.dma_start(out=wt_sb[:], in_=wt[0].rearrange("(p t) n -> p t n", t=QT))
 
         turned = psum.tile([P, CH, P], F32, name="turned")
@@ -86,7 +88,10 @@ def tile_attend_link_resid_topk_kernel(tc, qT, k_words, k_scales, kb, rt, ub, wt
             out=q_code[:].bitcast(FP8X4), scales=q_scale[:], in_=q_bf[:].rearrange("p t m j -> p (t m j)")
         )
 
-        k_code = keep.tile([P, N], U32, name="k_code", tag="reused", align_bytes=64)
+        ub_sb = keep.tile([P, QT], F32, name="ub_sb", tag="slot_qbf", align_bytes=64)
+        nc.sync.dma_start(out=ub_sb[:], in_=ub[0].rearrange("(p t) o -> p (t o)", t=QT))
+
+        k_code = keep.tile([P, N], U32, name="k_code", tag="slot_scales", align_bytes=64)
         nc.vector.tensor_copy(k_code[:], word_pool[:].bitcast(U32).indirect(offsets[:]))
 
         out_v = out[0].rearrange("(p t) n -> p t n", t=QT)
@@ -105,11 +110,11 @@ def tile_attend_link_resid_topk_kernel(tc, qT, k_words, k_scales, kb, rt, ub, wt
                 stop=True,
             )
         for t in range(QT):
+            nc.vector.tensor_tensor(out=unbiased[t][:], in0=rt_sb[:, t, :], in1=kb_all[:], op=SUB)
+        for t in range(QT):
             nc.vector.scalar_tensor_tensor(
-                out=unbiased[t][:], in0=rt_sb[:, t, :], scalar=ub_sb[:, t : t + 1], in1=kb_all[:], op0=SUB, op1=SUB
+                out=resid[t][:], in0=unbiased[t][:], scalar=ub_sb[:, t : t + 1], in1=acc[t][:], op0=SUB, op1=SUB
             )
-        for t in range(QT):
-            nc.vector.tensor_tensor(out=resid[t][:], in0=unbiased[t][:], in1=acc[t][:], op=SUB)
-        for t in range(QT):
-            nc.vector.tensor_tensor(out=res[t][:], in0=resid[t][:], in1=wt_sb[:, t, :], op=MULT)
-            nc.sync.dma_start(out=out_v[:, t, :], in_=res[t][:])
+        for t, cols in ((0, slice(0, N)), (1, slice(0, N // 2)), (1, slice(N // 2, N))):
+            nc.vector.tensor_tensor(out=res[t][:, cols], in0=resid[t][:, cols], in1=wt_sb[:, t, cols], op=MULT)
+            nc.sync.dma_start(out=out_v[:, t, cols], in_=res[t][:, cols])

@@ -31,6 +31,7 @@ def tile_attend_link_resid_topk_kernel(tc, qT, k_words, k_scales, kb, rt, ub, wt
     nc = tc.nc
     with ExitStack() as ctx:
         keep = ctx.enter_context(tc.tile_pool(name="keep", bufs=1))
+        reuse = ctx.enter_context(tc.tile_pool(name="reuse", bufs=1))
         psum = ctx.enter_context(tc.psum_pool(name="psum", bufs=1))
 
         offsets = keep.tile([P, N // 16], U16, name="offsets")
@@ -44,7 +45,7 @@ def tile_attend_link_resid_topk_kernel(tc, qT, k_words, k_scales, kb, rt, ub, wt
         warm_out = keep.tile([P, 1], F32, name="warm_out", tag="slot_rt")
         nc.scalar.copy(out=warm_out[:], in_=warm_in[:])
 
-        kb_pool = keep.tile([P, T], F32, name="kb_pool", tag="slot_kb", align_bytes=64)
+        kb_pool = reuse.tile([P, T], F32, name="kb_pool", align_bytes=64, offset=0)
         nc.vector.memset(kb_pool[:], 0.0)
         nc.sync.dma_start(out=kb_pool[0:1, :], in_=kb[0:1, :])
         scale_pool = keep.tile([P, T], U8, name="scale_pool", tag="slot_scales", align_bytes=64)
@@ -61,11 +62,12 @@ def tile_attend_link_resid_topk_kernel(tc, qT, k_words, k_scales, kb, rt, ub, wt
         nc.scalar.dma_start(out=rt_sb[:], in_=rt[0].rearrange("(p t) n -> p t n", t=QT))
 
         ident = keep.tile([P, P], F32, name="ident")
-        make_identity(nc, ident[:])
+        nc.vector.memset(ident[:], 0.0)
+        make_identity(nc, ident[:], nomemset=True)
 
         kb_row = keep.tile([P, N], F32, name="kb_row")
         nc.vector.tensor_copy(kb_row[:], kb_pool[:].indirect(offsets[:]))
-        k_scale = keep.tile([P, N], U8, name="k_scale", tag="slot_kb", align_bytes=64)
+        k_scale = reuse.tile([P, N], U8, name="k_scale", align_bytes=64, offset=0)
         nc.vector.tensor_copy(k_scale[:], scale_pool[:].indirect(offsets[:]))
 
         q_bf = keep.tile([P, QT, P, PACK], BF16, name="q_bf", tag="slot_qbf", align_bytes=64)
@@ -82,7 +84,7 @@ def tile_attend_link_resid_topk_kernel(tc, qT, k_words, k_scales, kb, rt, ub, wt
         for c in range(CH):
             nc.tensor.transpose(kb_all[:, c * P : (c + 1) * P], kb_col[:, c : c + 1].to_broadcast([P, P]), ident[:])
 
-        q_code = keep.tile([P, NQ], U32, name="q_code", align_bytes=64)
+        q_code = reuse.tile([P, NQ], U32, name="q_code", align_bytes=64, offset=N)
         q_scale = keep.tile([P, NQ], U8, name="q_scale", align_bytes=64)
         nc.vector.quantize_mx(
             out=q_code[:].bitcast(FP8X4), scales=q_scale[:], in_=q_bf[:].rearrange("p t m j -> p (t m j)")

@@ -22,6 +22,7 @@ T = 2048
 QT = NQ // P
 QUAD = 32
 CH = N // P
+HALF = N // 2
 
 FLOPS = 2 * D * NQ * N
 BYTES = 4 * D * NQ + D * T + (D // 32) * T + 4 * T + 3 * 4 * NQ * N + 4 * NQ + 2 * P * (N // 16)
@@ -37,16 +38,16 @@ def tile_attend_link_resid_topk_kernel(tc, qT, k_words, k_scales, kb, rt, ub, wt
         offsets = keep.tile([P, N // 16], U16, name="offsets")
         nc.sync.dma_start(offsets[:], offs)
 
-        q_raw = keep.tile([P, PACK, NQ], F32, name="q_raw", tag="slot_q")
-        nc.sync.dma_start(out=q_raw[:], in_=qT[0].rearrange("(p j) w -> p j w", j=PACK))
+        q_raw = keep.tile([P, PACK, NQ], F32, name="q_raw")
+        nc.scalar.dma_start(out=q_raw[:], in_=qT[0].rearrange("(p j) w -> p j w", j=PACK))
 
-        warm_in = keep.tile([P, 1], F32, name="warm_in", tag="slot_words")
+        warm_in = keep.tile([P, 1], F32, name="warm_in")
         nc.vector.memset(warm_in[:], 0.0)
-        warm_out = keep.tile([P, 1], F32, name="warm_out", tag="slot_rt")
+        warm_out = keep.tile([P, 1], F32, name="warm_out")
         nc.scalar.copy(out=warm_out[:], in_=warm_in[:])
 
         kb_pool = reuse.tile([P, T], F32, name="kb_pool", align_bytes=64, offset=0)
-        nc.vector.memset(kb_pool[:], 0.0)
+        nc.vector.memset(kb_pool[:].bitcast(I32), 0)
         nc.sync.dma_start(out=kb_pool[0:1, :], in_=kb[0:1, :])
         scale_pool = keep.tile([P, T], U8, name="scale_pool", tag="slot_scales", align_bytes=64)
         nc.vector.memset(scale_pool[:].bitcast(I32), 0)
@@ -56,35 +57,41 @@ def tile_attend_link_resid_topk_kernel(tc, qT, k_words, k_scales, kb, rt, ub, wt
                 in_=k_scales[0, PACK * quad : PACK * (quad + 1), :].bitcast(I32),
             )
 
-        word_pool = keep.tile([P, T], I32, name="word_pool", tag="slot_words")
-        nc.scalar.dma_start(out=word_pool[:], in_=k_words[0].rearrange("p n r -> p (n r)").bitcast(I32))
-        rt_sb = keep.tile([P, QT, N], F32, name="rt_sb", tag="slot_rt")
-        nc.scalar.dma_start(out=rt_sb[:], in_=rt[0].rearrange("(p t) n -> p t n", t=QT))
-
+        zeros = keep.tile([P, P], F32, name="zeros", tag="slot_words")
+        nc.vector.memset(zeros[:], 0.0)
         ident = keep.tile([P, P], F32, name="ident")
-        nc.vector.memset(ident[:], 0.0)
+        nc.vector.tensor_copy(ident[:], zeros[:])
         make_identity(nc, ident[:], nomemset=True)
+
+        word_pool = keep.tile([P, T], I32, name="word_pool", tag="slot_words")
+        nc.sync.dma_start(out=word_pool[:], in_=k_words[0].rearrange("p n r -> p (n r)").bitcast(I32))
 
         kb_row = keep.tile([P, N], F32, name="kb_row")
         nc.vector.tensor_copy(kb_row[:], kb_pool[:].indirect(offsets[:]))
-        k_scale = reuse.tile([P, N], U8, name="k_scale", align_bytes=64, offset=0)
+        k_scale = keep.tile([P, N], U8, name="k_scale", align_bytes=64)
         nc.vector.tensor_copy(k_scale[:], scale_pool[:].indirect(offsets[:]))
 
         q_bf = keep.tile([P, QT, P, PACK], BF16, name="q_bf", tag="slot_qbf", align_bytes=64)
         nc.scalar.copy(out=q_bf[:], in_=q_raw[:].rearrange("p j (m t) -> p t m j", t=QT))
-        wt_sb = keep.tile([P, QT, N], F32, name="wt_sb", tag="slot_q")
-        nc.scalar.dma_start(out=wt_sb[:], in_=wt[0].rearrange("(p t) n -> p t n", t=QT))
+        rt_v = rt[0].rearrange("(p t) n -> p t n", t=QT)
+        rt_sb = [reuse.tile([P, N], F32, name=f"rt_sb{t}", align_bytes=64, offset=4 * N * (t + 1)) for t in range(QT)]
+        for t in range(QT):
+            nc.sync.dma_start(out=rt_sb[t][:], in_=rt_v[:, t, :])
+        wt_sb = reuse.tile([P, QT, N], F32, name="wt_sb", align_bytes=64, offset=4 * N * (QT + 1))
+        nc.sync.dma_start(out=wt_sb[:], in_=wt[0].rearrange("(p t) n -> p t n", t=QT))
 
-        turned = psum.tile([P, CH, P], F32, name="turned")
-        for c in range(CH):
-            nc.tensor.transpose(turned[:, c, :], kb_row[:, c * P : (c + 1) * P], ident[:])
         kb_col = keep.tile([P, CH], F32, name="kb_col")
-        nc.scalar.copy(out=kb_col[:], in_=turned[:, :, 0])
+        for h in range(2):
+            turned = psum.tile([P, CH // 2, P], F32, name=f"turned{h}")
+            for c in range(CH // 2):
+                first = (h * CH // 2 + c) * P
+                nc.tensor.transpose(turned[:, c, :], kb_row[:, first : first + P], ident[:])
+            nc.scalar.copy(out=kb_col[:, h * CH // 2 : (h + 1) * CH // 2], in_=turned[:, :, 0])
         kb_all = psum.tile([P, N], F32, name="kb_all")
         for c in range(CH):
             nc.tensor.transpose(kb_all[:, c * P : (c + 1) * P], kb_col[:, c : c + 1].to_broadcast([P, P]), ident[:])
 
-        q_code = reuse.tile([P, NQ], U32, name="q_code", align_bytes=64, offset=N)
+        q_code = reuse.tile([P, NQ], U32, name="q_code", align_bytes=64, offset=0)
         q_scale = keep.tile([P, NQ], U8, name="q_scale", align_bytes=64)
         nc.vector.quantize_mx(
             out=q_code[:].bitcast(FP8X4), scales=q_scale[:], in_=q_bf[:].rearrange("p t m j -> p (t m j)")
@@ -94,29 +101,37 @@ def tile_attend_link_resid_topk_kernel(tc, qT, k_words, k_scales, kb, rt, ub, wt
         nc.sync.dma_start(out=ub_sb[:], in_=ub[0].rearrange("(p t) o -> p (t o)", t=QT))
 
         k_code = keep.tile([P, N], U32, name="k_code", tag="slot_scales", align_bytes=64)
-        nc.vector.tensor_copy(k_code[:], word_pool[:].bitcast(U32).indirect(offsets[:]))
+        acc = [psum.tile([P, N], F32, name=f"acc{t}") for t in range(QT)]
+        for h in range(2):
+            cols = slice(h * HALF, (h + 1) * HALF)
+            listed = offsets[:, h * HALF // 16 : (h + 1) * HALF // 16]
+            nc.vector.tensor_copy(k_code[:, cols], word_pool[:].bitcast(U32).indirect(listed))
+            for t in range(QT):
+                nc.tensor.matmul_mx(
+                    out=acc[t][:, cols],
+                    lhsT=q_code[:, t * P : (t + 1) * P].bitcast(FP8X4),
+                    lhsT_scale=q_scale[:, t * P : (t + 1) * P],
+                    rhs=k_code[:, cols].bitcast(FP8X4),
+                    rhs_scale=k_scale[:, cols],
+                    start=True,
+                    stop=True,
+                )
 
         out_v = out[0].rearrange("(p t) n -> p t n", t=QT)
-        acc = [psum.tile([P, N], F32, name=f"acc{t}") for t in range(QT)]
         unbiased = [keep.tile([P, N], F32, name=f"unbiased{t}") for t in range(QT)]
         resid = [keep.tile([P, N], F32, name=f"resid{t}") for t in range(QT)]
         res = [keep.tile([P, N], F32, name=f"res{t}") for t in range(QT)]
         for t in range(QT):
-            nc.tensor.matmul_mx(
-                out=acc[t][:],
-                lhsT=q_code[:, t * P : (t + 1) * P].bitcast(FP8X4),
-                lhsT_scale=q_scale[:, t * P : (t + 1) * P],
-                rhs=k_code[:].bitcast(FP8X4),
-                rhs_scale=k_scale[:],
-                start=True,
-                stop=True,
-            )
+            nc.vector.tensor_tensor(out=unbiased[t][:], in0=rt_sb[t][:], in1=kb_all[:], op=SUB)
         for t in range(QT):
-            nc.vector.tensor_tensor(out=unbiased[t][:], in0=rt_sb[:, t, :], in1=kb_all[:], op=SUB)
-        for t in range(QT):
+            nc.vector.tensor_tensor(out=resid[t][:], in0=unbiased[t][:], in1=acc[t][:], op=SUB)
+        for t, cols in ((0, slice(0, N)), (1, slice(0, HALF)), (1, slice(HALF, N))):
             nc.vector.scalar_tensor_tensor(
-                out=resid[t][:], in0=unbiased[t][:], scalar=ub_sb[:, t : t + 1], in1=acc[t][:], op0=SUB, op1=SUB
+                out=res[t][:, cols],
+                in0=resid[t][:, cols],
+                scalar=ub_sb[:, t : t + 1],
+                in1=wt_sb[:, t, cols],
+                op0=SUB,
+                op1=MULT,
             )
-        for t, cols in ((0, slice(0, N)), (1, slice(0, N // 2)), (1, slice(N // 2, N))):
-            nc.vector.tensor_tensor(out=res[t][:, cols], in0=resid[t][:, cols], in1=wt_sb[:, t, cols], op=MULT)
             nc.sync.dma_start(out=out_v[:, t, cols], in_=res[t][:, cols])

@@ -23,6 +23,8 @@ QT = NQ // P
 QUAD = 32
 CH = N // P
 HALF = N // 2
+KB_ROW = P - 1
+LATE_WORDS = T + 2 * QT * N + 16
 
 FLOPS = 2 * D * NQ * N
 BYTES = 4 * D * NQ + D * T + (D // 32) * T + 4 * T + 3 * 4 * NQ * N + 4 * NQ + 2 * P * (N // 16)
@@ -32,11 +34,13 @@ def tile_attend_link_resid_topk_kernel(tc, qT, k_words, k_scales, kb, rt, ub, wt
     nc = tc.nc
     with ExitStack() as ctx:
         keep = ctx.enter_context(tc.tile_pool(name="keep", bufs=1))
-        reuse = ctx.enter_context(tc.tile_pool(name="reuse", bufs=1))
+        late = ctx.enter_context(tc.tile_pool(name="late", bufs=1))
         psum = ctx.enter_context(tc.psum_pool(name="psum", bufs=1))
 
         offsets = keep.tile([P, N // 16], U16, name="offsets")
         nc.sync.dma_start(offsets[:], offs)
+        kb_pool = keep.tile([P, T], F32, name="kb_pool", align_bytes=64)
+        nc.sync.dma_start(out=kb_pool[KB_ROW:P, :], in_=kb[0:1, :])
 
         q_raw = keep.tile([P, PACK, NQ], F32, name="q_raw")
         nc.scalar.dma_start(out=q_raw[:], in_=qT[0].rearrange("(p j) w -> p j w", j=PACK))
@@ -46,9 +50,8 @@ def tile_attend_link_resid_topk_kernel(tc, qT, k_words, k_scales, kb, rt, ub, wt
         warm_out = keep.tile([P, 1], F32, name="warm_out")
         nc.scalar.copy(out=warm_out[:], in_=warm_in[:])
 
-        kb_pool = reuse.tile([P, T], F32, name="kb_pool", align_bytes=64, offset=0)
-        nc.vector.memset(kb_pool[:].bitcast(I32), 0)
-        nc.sync.dma_start(out=kb_pool[0:1, :], in_=kb[0:1, :])
+        zeros = late.tile([P, LATE_WORDS], F32, name="zeros", align_bytes=64, offset=0)
+        nc.vector.memset(zeros[:, :P], 0.0)
         scale_pool = keep.tile([P, T], U8, name="scale_pool", tag="slot_scales", align_bytes=64)
         nc.vector.memset(scale_pool[:].bitcast(I32), 0)
         for quad in range(P // QUAD):
@@ -57,50 +60,50 @@ def tile_attend_link_resid_topk_kernel(tc, qT, k_words, k_scales, kb, rt, ub, wt
                 in_=k_scales[0, PACK * quad : PACK * (quad + 1), :].bitcast(I32),
             )
 
-        zeros = keep.tile([P, P], F32, name="zeros", tag="slot_words")
-        nc.vector.memset(zeros[:], 0.0)
         ident = keep.tile([P, P], F32, name="ident")
-        nc.vector.tensor_copy(ident[:], zeros[:])
+        nc.vector.tensor_copy(ident[:], zeros[:, :P])
         make_identity(nc, ident[:], nomemset=True)
+        nc.vector.memset(kb_pool[0:KB_ROW, :].bitcast(I32), 0)
 
-        word_pool = keep.tile([P, T], I32, name="word_pool", tag="slot_words")
+        word_pool = late.tile([P, T], I32, name="word_pool", align_bytes=64, offset=0)
         nc.sync.dma_start(out=word_pool[:], in_=k_words[0].rearrange("p n r -> p (n r)").bitcast(I32))
+        ub_sb = late.tile([P, QT], F32, name="ub_sb", align_bytes=64, offset=4 * (T + 2 * QT * N))
+        with nc.allow_non_contiguous_dma(reason="one bias a partition and query tile"):
+            nc.sync.dma_start(out=ub_sb[:], in_=ub[0].rearrange("(t p) o -> p (t o)", t=QT))
+        rt_sb = [late.tile([P, N], F32, name=f"rt_sb{t}", align_bytes=64, offset=4 * (T + t * N)) for t in range(QT)]
+        wt_sb = [
+            late.tile([P, N], F32, name=f"wt_sb{t}", align_bytes=64, offset=4 * (T + (QT + t) * N)) for t in range(QT)
+        ]
+        for t in range(QT):
+            nc.sync.dma_start(out=rt_sb[t][:], in_=rt[0, t * P : (t + 1) * P, :])
+        for t in range(QT):
+            nc.sync.dma_start(out=wt_sb[t][:], in_=wt[0, t * P : (t + 1) * P, :])
 
         kb_row = keep.tile([P, N], F32, name="kb_row")
         nc.vector.tensor_copy(kb_row[:], kb_pool[:].indirect(offsets[:]))
         k_scale = keep.tile([P, N], U8, name="k_scale", align_bytes=64)
         nc.vector.tensor_copy(k_scale[:], scale_pool[:].indirect(offsets[:]))
 
-        q_bf = keep.tile([P, QT, P, PACK], BF16, name="q_bf", tag="slot_qbf", align_bytes=64)
-        nc.scalar.copy(out=q_bf[:], in_=q_raw[:].rearrange("p j (m t) -> p t m j", t=QT))
-        rt_v = rt[0].rearrange("(p t) n -> p t n", t=QT)
-        rt_sb = [reuse.tile([P, N], F32, name=f"rt_sb{t}", align_bytes=64, offset=4 * N * (t + 1)) for t in range(QT)]
-        for t in range(QT):
-            nc.sync.dma_start(out=rt_sb[t][:], in_=rt_v[:, t, :])
-        wt_sb = reuse.tile([P, QT, N], F32, name="wt_sb", align_bytes=64, offset=4 * N * (QT + 1))
-        nc.sync.dma_start(out=wt_sb[:], in_=wt[0].rearrange("(p t) n -> p t n", t=QT))
+        q_bf = keep.tile([P, NQ, PACK], BF16, name="q_bf", align_bytes=64)
+        nc.scalar.copy(
+            out=q_bf[:].rearrange("p (c i) j -> p c j i", i=PACK),
+            in_=q_raw[:].rearrange("p j (c i) -> p c j i", i=PACK),
+        )
 
         kb_col = keep.tile([P, CH], F32, name="kb_col")
-        for h in range(2):
-            turned = psum.tile([P, CH // 2, P], F32, name=f"turned{h}")
-            for c in range(CH // 2):
-                first = (h * CH // 2 + c) * P
-                nc.tensor.transpose(turned[:, c, :], kb_row[:, first : first + P], ident[:])
-            nc.scalar.copy(out=kb_col[:, h * CH // 2 : (h + 1) * CH // 2], in_=turned[:, :, 0])
+        turned = psum.tile([P, CH, P], F32, name="turned")
+        for c in range(CH):
+            nc.tensor.transpose(turned[:, c, :], kb_row[:, c * P : (c + 1) * P], ident[:])
+        nc.scalar.copy(out=kb_col[:], in_=turned[:, :, KB_ROW])
         kb_all = psum.tile([P, N], F32, name="kb_all")
         for c in range(CH):
             nc.tensor.transpose(kb_all[:, c * P : (c + 1) * P], kb_col[:, c : c + 1].to_broadcast([P, P]), ident[:])
 
-        q_code = reuse.tile([P, NQ], U32, name="q_code", align_bytes=64, offset=0)
+        q_code = keep.tile([P, NQ], U32, name="q_code", tag="slot_scales", align_bytes=64)
         q_scale = keep.tile([P, NQ], U8, name="q_scale", align_bytes=64)
-        nc.vector.quantize_mx(
-            out=q_code[:].bitcast(FP8X4), scales=q_scale[:], in_=q_bf[:].rearrange("p t m j -> p (t m j)")
-        )
+        nc.vector.quantize_mx(out=q_code[:].bitcast(FP8X4), scales=q_scale[:], in_=q_bf[:].rearrange("p m j -> p (m j)"))
 
-        ub_sb = keep.tile([P, QT], F32, name="ub_sb", tag="slot_qbf", align_bytes=64)
-        nc.sync.dma_start(out=ub_sb[:], in_=ub[0].rearrange("(p t) o -> p (t o)", t=QT))
-
-        k_code = keep.tile([P, N], U32, name="k_code", tag="slot_scales", align_bytes=64)
+        k_code = keep.tile([P, N], U32, name="k_code", align_bytes=64)
         acc = [psum.tile([P, N], F32, name=f"acc{t}") for t in range(QT)]
         for h in range(2):
             cols = slice(h * HALF, (h + 1) * HALF)
@@ -117,7 +120,6 @@ def tile_attend_link_resid_topk_kernel(tc, qT, k_words, k_scales, kb, rt, ub, wt
                     stop=True,
                 )
 
-        out_v = out[0].rearrange("(p t) n -> p t n", t=QT)
         unbiased = [keep.tile([P, N], F32, name=f"unbiased{t}") for t in range(QT)]
         resid = [keep.tile([P, N], F32, name=f"resid{t}") for t in range(QT)]
         res = [keep.tile([P, N], F32, name=f"res{t}") for t in range(QT)]
@@ -130,8 +132,8 @@ def tile_attend_link_resid_topk_kernel(tc, qT, k_words, k_scales, kb, rt, ub, wt
                 out=res[t][:, cols],
                 in0=resid[t][:, cols],
                 scalar=ub_sb[:, t : t + 1],
-                in1=wt_sb[:, t, cols],
+                in1=wt_sb[t][:, cols],
                 op0=SUB,
                 op1=MULT,
             )
-            nc.sync.dma_start(out=out_v[:, t, cols], in_=res[t][:, cols])
+            nc.sync.dma_start(out=out[0, t * P : (t + 1) * P, cols], in_=res[t][:, cols])

@@ -35,6 +35,7 @@ def tile_attend_link_resid_topk_kernel(tc, qT, k_words, k_scales, kb, rt, ub, wt
     with ExitStack() as ctx:
         keep = ctx.enter_context(tc.tile_pool(name="keep", bufs=1))
         late = ctx.enter_context(tc.tile_pool(name="late", bufs=1))
+        rows = ctx.enter_context(tc.tile_pool(name="rows", bufs=1))
         psum = ctx.enter_context(tc.psum_pool(name="psum", bufs=1))
 
         offsets = keep.tile([P, N // 16], U16, name="offsets")
@@ -52,7 +53,7 @@ def tile_attend_link_resid_topk_kernel(tc, qT, k_words, k_scales, kb, rt, ub, wt
 
         zeros = late.tile([P, LATE_WORDS], F32, name="zeros", align_bytes=64, offset=0)
         nc.vector.memset(zeros[:, :P], 0.0)
-        scale_pool = keep.tile([P, T], U8, name="scale_pool", tag="slot_scales", align_bytes=64)
+        scale_pool = keep.tile([P, T], U8, name="scale_pool", align_bytes=64)
         nc.vector.memset(scale_pool[:].bitcast(I32), 0)
         for quad in range(P // QUAD):
             nc.sync.dma_start(
@@ -79,7 +80,7 @@ def tile_attend_link_resid_topk_kernel(tc, qT, k_words, k_scales, kb, rt, ub, wt
         for t in range(QT):
             nc.sync.dma_start(out=wt_sb[t][:], in_=wt[0, t * P : (t + 1) * P, :])
 
-        kb_row = keep.tile([P, N], F32, name="kb_row")
+        kb_row = rows.tile([P, N], F32, name="kb_row", align_bytes=64, offset=64)
         nc.vector.tensor_copy(kb_row[:], kb_pool[:].indirect(offsets[:]))
         k_scale = keep.tile([P, N], U8, name="k_scale", align_bytes=64)
         nc.vector.tensor_copy(k_scale[:], scale_pool[:].indirect(offsets[:]))
@@ -99,19 +100,19 @@ def tile_attend_link_resid_topk_kernel(tc, qT, k_words, k_scales, kb, rt, ub, wt
         for c in range(CH):
             nc.tensor.transpose(kb_all[:, c * P : (c + 1) * P], kb_col[:, c : c + 1].to_broadcast([P, P]), ident[:])
 
-        q_code = keep.tile([P, NQ], U32, name="q_code", tag="slot_scales", align_bytes=64)
-        q_scale = keep.tile([P, NQ], U8, name="q_scale", align_bytes=64)
+        q_code = keep.tile([P, NQ], U32, name="q_code", align_bytes=64)
+        q_scale = rows.tile([P, NQ], U8, name="q_scale", align_bytes=64, offset=0)
         nc.vector.quantize_mx(out=q_code[:].bitcast(FP8X4), scales=q_scale[:], in_=q_bf[:].rearrange("p m j -> p (m j)"))
 
-        k_code = keep.tile([P, N], U32, name="k_code", align_bytes=64)
-        acc = [psum.tile([P, N], F32, name=f"acc{t}") for t in range(QT)]
+        k_code = rows.tile([P, N], U32, name="k_code", align_bytes=64, offset=NQ)
+        acc = [[psum.tile([P, HALF], F32, name=f"acc{t}_{h}") for h in range(2)] for t in range(QT)]
         for h in range(2):
             cols = slice(h * HALF, (h + 1) * HALF)
             listed = offsets[:, h * HALF // 16 : (h + 1) * HALF // 16]
             nc.vector.tensor_copy(k_code[:, cols], word_pool[:].bitcast(U32).indirect(listed))
             for t in range(QT):
                 nc.tensor.matmul_mx(
-                    out=acc[t][:, cols],
+                    out=acc[t][h][:],
                     lhsT=q_code[:, t * P : (t + 1) * P].bitcast(FP8X4),
                     lhsT_scale=q_scale[:, t * P : (t + 1) * P],
                     rhs=k_code[:, cols].bitcast(FP8X4),
@@ -123,17 +124,19 @@ def tile_attend_link_resid_topk_kernel(tc, qT, k_words, k_scales, kb, rt, ub, wt
         unbiased = [keep.tile([P, N], F32, name=f"unbiased{t}") for t in range(QT)]
         resid = [keep.tile([P, N], F32, name=f"resid{t}") for t in range(QT)]
         res = [keep.tile([P, N], F32, name=f"res{t}") for t in range(QT)]
+        halves = (slice(0, HALF), slice(HALF, N))
         for t in range(QT):
             nc.vector.tensor_tensor(out=unbiased[t][:], in0=rt_sb[t][:], in1=kb_all[:], op=SUB)
         for t in range(QT):
-            nc.vector.tensor_tensor(out=resid[t][:], in0=unbiased[t][:], in1=acc[t][:], op=SUB)
-        for t, cols in ((0, slice(0, N)), (1, slice(0, HALF)), (1, slice(HALF, N))):
-            nc.vector.scalar_tensor_tensor(
-                out=res[t][:, cols],
-                in0=resid[t][:, cols],
-                scalar=ub_sb[:, t : t + 1],
-                in1=wt_sb[t][:, cols],
-                op0=SUB,
-                op1=MULT,
-            )
-            nc.sync.dma_start(out=out[0, t * P : (t + 1) * P, cols], in_=res[t][:, cols])
+            for h, cols in enumerate(halves):
+                nc.vector.tensor_tensor(out=resid[t][:, cols], in0=unbiased[t][:, cols], in1=acc[t][h][:], op=SUB)
+            for cols in halves:
+                nc.vector.scalar_tensor_tensor(
+                    out=res[t][:, cols],
+                    in0=resid[t][:, cols],
+                    scalar=ub_sb[:, t : t + 1],
+                    in1=wt_sb[t][:, cols],
+                    op0=SUB,
+                    op1=MULT,
+                )
+                nc.sync.dma_start(out=out[0, t * P : (t + 1) * P, cols], in_=res[t][:, cols])

@@ -24,6 +24,7 @@ QUAD = 32
 CH = N // P
 HALF = N // 2
 KB_ROW = P - 1
+KB_POOL_COLS = 1368
 LATE_WORDS = T + 2 * QT * N + 16
 
 FLOPS = 2 * D * NQ * N
@@ -35,13 +36,16 @@ def tile_attend_link_resid_topk_kernel(tc, qT, k_words, k_scales, kb, rt, ub, wt
     with ExitStack() as ctx:
         keep = ctx.enter_context(tc.tile_pool(name="keep", bufs=1))
         late = ctx.enter_context(tc.tile_pool(name="late", bufs=1))
+        window = ctx.enter_context(tc.tile_pool(name="window", bufs=1))
         rows = ctx.enter_context(tc.tile_pool(name="rows", bufs=1))
         psum = ctx.enter_context(tc.psum_pool(name="psum", bufs=1))
 
         offsets = keep.tile([P, N // 16], U16, name="offsets")
         nc.sync.dma_start(offsets[:], offs)
-        kb_pool = keep.tile([P, T], F32, name="kb_pool", align_bytes=64)
-        nc.sync.dma_start(out=kb_pool[KB_ROW:P, :], in_=kb[0:1, :])
+        kb_pool = window.tile([P, T + 1], F32, name="kb_pool", align_bytes=64, offset=0)
+        nc.scalar.dma_start(out=kb_pool[KB_ROW:P, :T], in_=kb[0:1, :])
+
+        nc.gpsimd.memset(kb_pool[0:KB_ROW, :KB_POOL_COLS].bitcast(I32), 0)
 
         q_raw = keep.tile([P, PACK, NQ], F32, name="q_raw")
         nc.scalar.dma_start(out=q_raw[:], in_=qT[0].rearrange("(p j) w -> p j w", j=PACK))
@@ -52,19 +56,19 @@ def tile_attend_link_resid_topk_kernel(tc, qT, k_words, k_scales, kb, rt, ub, wt
         nc.scalar.copy(out=warm_out[:], in_=warm_in[:])
 
         zeros = late.tile([P, LATE_WORDS], F32, name="zeros", align_bytes=64, offset=0)
-        nc.vector.memset(zeros[:, :P], 0.0)
-        scale_pool = keep.tile([P, T], U8, name="scale_pool", align_bytes=64)
+        nc.vector.memset(zeros[:, : P + 1], 0.0)
+        scale_pool = keep.tile([P, T + 4], U8, name="scale_pool", align_bytes=64)
         nc.vector.memset(scale_pool[:].bitcast(I32), 0)
         for quad in range(P // QUAD):
             nc.sync.dma_start(
-                out=scale_pool[QUAD * quad : QUAD * quad + PACK, :].bitcast(I32),
+                out=scale_pool[QUAD * quad : QUAD * quad + PACK, :T].bitcast(I32),
                 in_=k_scales[0, PACK * quad : PACK * (quad + 1), :].bitcast(I32),
             )
 
         ident = keep.tile([P, P], F32, name="ident")
-        nc.vector.tensor_copy(ident[:], zeros[:, :P])
+        nc.vector.tensor_tensor(out=ident[:], in0=zeros[:, :P], in1=zeros[:, 1 : P + 1], op=SUB)
         make_identity(nc, ident[:], nomemset=True)
-        nc.vector.memset(kb_pool[0:KB_ROW, :].bitcast(I32), 0)
+        nc.vector.memset(kb_pool[0:KB_ROW, KB_POOL_COLS : T + 1].bitcast(I32), 0)
 
         word_pool = late.tile([P, T], I32, name="word_pool", align_bytes=64, offset=0)
         nc.sync.dma_start(out=word_pool[:], in_=k_words[0].rearrange("p n r -> p (n r)").bitcast(I32))
@@ -81,9 +85,9 @@ def tile_attend_link_resid_topk_kernel(tc, qT, k_words, k_scales, kb, rt, ub, wt
             nc.sync.dma_start(out=wt_sb[t][:], in_=wt[0, t * P : (t + 1) * P, :])
 
         kb_row = rows.tile([P, N], F32, name="kb_row", align_bytes=64, offset=64)
-        nc.vector.tensor_copy(kb_row[:], kb_pool[:].indirect(offsets[:]))
-        k_scale = keep.tile([P, N], U8, name="k_scale", align_bytes=64)
-        nc.vector.tensor_copy(k_scale[:], scale_pool[:].indirect(offsets[:]))
+        nc.vector.tensor_copy(kb_row[:], kb_pool[:, :T].indirect(offsets[:]))
+        k_scale = window.tile([P, N], U8, name="k_scale", align_bytes=64, offset=4 * (NQ + N))
+        nc.vector.tensor_copy(k_scale[:], scale_pool[:, :T].indirect(offsets[:]))
 
         q_bf = keep.tile([P, NQ, PACK], BF16, name="q_bf", align_bytes=64)
         nc.scalar.copy(
@@ -95,24 +99,24 @@ def tile_attend_link_resid_topk_kernel(tc, qT, k_words, k_scales, kb, rt, ub, wt
         turned = psum.tile([P, CH, P], F32, name="turned")
         for c in range(CH):
             nc.tensor.transpose(turned[:, c, :], kb_row[:, c * P : (c + 1) * P], ident[:])
-        nc.scalar.copy(out=kb_col[:], in_=turned[:, :, KB_ROW])
+        nc.vector.tensor_copy(kb_col[:], turned[:, :, KB_ROW])
         kb_all = psum.tile([P, N], F32, name="kb_all")
         for c in range(CH):
             nc.tensor.transpose(kb_all[:, c * P : (c + 1) * P], kb_col[:, c : c + 1].to_broadcast([P, P]), ident[:])
 
-        q_code = keep.tile([P, NQ], U32, name="q_code", align_bytes=64)
+        q_code = window.tile([P, NQ], U32, name="q_code", align_bytes=64, offset=0)
         q_scale = rows.tile([P, NQ], U8, name="q_scale", align_bytes=64, offset=0)
         nc.vector.quantize_mx(out=q_code[:].bitcast(FP8X4), scales=q_scale[:], in_=q_bf[:].rearrange("p m j -> p (m j)"))
 
         k_code = rows.tile([P, N], U32, name="k_code", align_bytes=64, offset=NQ)
-        acc = [[psum.tile([P, HALF], F32, name=f"acc{t}_{h}") for h in range(2)] for t in range(QT)]
+        acc = [psum.tile([P, N], F32, name=f"acc{t}") for t in range(QT)]
         for h in range(2):
             cols = slice(h * HALF, (h + 1) * HALF)
             listed = offsets[:, h * HALF // 16 : (h + 1) * HALF // 16]
             nc.vector.tensor_copy(k_code[:, cols], word_pool[:].bitcast(U32).indirect(listed))
             for t in range(QT):
                 nc.tensor.matmul_mx(
-                    out=acc[t][h][:],
+                    out=acc[t][:, cols],
                     lhsT=q_code[:, t * P : (t + 1) * P].bitcast(FP8X4),
                     lhsT_scale=q_scale[:, t * P : (t + 1) * P],
                     rhs=k_code[:, cols].bitcast(FP8X4),
@@ -124,19 +128,17 @@ def tile_attend_link_resid_topk_kernel(tc, qT, k_words, k_scales, kb, rt, ub, wt
         unbiased = [keep.tile([P, N], F32, name=f"unbiased{t}") for t in range(QT)]
         resid = [keep.tile([P, N], F32, name=f"resid{t}") for t in range(QT)]
         res = [keep.tile([P, N], F32, name=f"res{t}") for t in range(QT)]
-        halves = (slice(0, HALF), slice(HALF, N))
         for t in range(QT):
             nc.vector.tensor_tensor(out=unbiased[t][:], in0=rt_sb[t][:], in1=kb_all[:], op=SUB)
         for t in range(QT):
-            for h, cols in enumerate(halves):
-                nc.vector.tensor_tensor(out=resid[t][:, cols], in0=unbiased[t][:, cols], in1=acc[t][h][:], op=SUB)
-            for cols in halves:
-                nc.vector.scalar_tensor_tensor(
-                    out=res[t][:, cols],
-                    in0=resid[t][:, cols],
-                    scalar=ub_sb[:, t : t + 1],
-                    in1=wt_sb[t][:, cols],
-                    op0=SUB,
-                    op1=MULT,
-                )
-                nc.sync.dma_start(out=out[0, t * P : (t + 1) * P, cols], in_=res[t][:, cols])
+            nc.vector.tensor_tensor(out=resid[t][:], in0=unbiased[t][:], in1=acc[t][:], op=SUB)
+        for t, cols in ((0, slice(0, N)), (1, slice(0, HALF)), (1, slice(HALF, N))):
+            nc.vector.scalar_tensor_tensor(
+                out=res[t][:, cols],
+                in0=resid[t][:, cols],
+                scalar=ub_sb[:, t : t + 1],
+                in1=wt_sb[t][:, cols],
+                op0=SUB,
+                op1=MULT,
+            )
+            nc.sync.dma_start(out=out[0, t * P : (t + 1) * P, cols], in_=res[t][:, cols])

@@ -25,7 +25,7 @@ CH = N // P
 HALF = N // 2
 KB_ROW = P - 1
 KB_POOL_COLS = 1368
-LATE_WORDS = T + 2 * QT * N + 16
+LATE_WORDS = T + 2 * QT * N
 
 FLOPS = 2 * D * NQ * N
 BYTES = 4 * D * NQ + D * T + (D // 32) * T + 4 * T + 3 * 4 * NQ * N + 4 * NQ + 2 * P * (N // 16)
@@ -68,13 +68,13 @@ def tile_attend_link_resid_topk_kernel(tc, qT, k_words, k_scales, kb, rt, ub, wt
         ident = keep.tile([P, P], F32, name="ident")
         nc.vector.tensor_tensor(out=ident[:], in0=zeros[:, :P], in1=zeros[:, 1 : P + 1], op=SUB)
         make_identity(nc, ident[:], nomemset=True)
+        ub_rows = keep.tile([P, P], F32, name="ub_rows")
+        nc.vector.tensor_tensor(out=ub_rows[:], in0=zeros[:, :P], in1=zeros[:, 1 : P + 1], op=SUB)
         nc.vector.memset(kb_pool[0:KB_ROW, KB_POOL_COLS : T + 1].bitcast(I32), 0)
 
         word_pool = late.tile([P, T], I32, name="word_pool", align_bytes=64, offset=0)
         nc.sync.dma_start(out=word_pool[:], in_=k_words[0].rearrange("p n r -> p (n r)").bitcast(I32))
-        ub_sb = late.tile([P, QT], F32, name="ub_sb", align_bytes=64, offset=4 * (T + 2 * QT * N))
-        with nc.allow_non_contiguous_dma(reason="one bias a partition and query tile"):
-            nc.sync.dma_start(out=ub_sb[:], in_=ub[0].rearrange("(t p) o -> p (t o)", t=QT))
+        nc.sync.dma_start(out=ub_rows[0:QT, :], in_=ub[0].rearrange("(t p) o -> t (p o)", t=QT))
         rt_sb = [late.tile([P, N], F32, name=f"rt_sb{t}", align_bytes=64, offset=4 * (T + t * N)) for t in range(QT)]
         wt_sb = [
             late.tile([P, N], F32, name=f"wt_sb{t}", align_bytes=64, offset=4 * (T + (QT + t) * N)) for t in range(QT)
@@ -104,19 +104,24 @@ def tile_attend_link_resid_topk_kernel(tc, qT, k_words, k_scales, kb, rt, ub, wt
         for c in range(CH):
             nc.tensor.transpose(kb_all[:, c * P : (c + 1) * P], kb_col[:, c : c + 1].to_broadcast([P, P]), ident[:])
 
+        kb_sb = keep.tile([P, HALF], F32, name="kb_sb")
+        nc.scalar.copy(out=kb_sb[:], in_=kb_all[:, :HALF])
+        ub_turned = psum.tile([P, CH, P], F32, name="ub_turned", tag="turned")[:, 0, :]
+        nc.tensor.transpose(ub_turned, ub_rows[:], ident[:])
+
         q_code = window.tile([P, NQ], U32, name="q_code", align_bytes=64, offset=0)
         q_scale = rows.tile([P, NQ], U8, name="q_scale", align_bytes=64, offset=0)
         nc.vector.quantize_mx(out=q_code[:].bitcast(FP8X4), scales=q_scale[:], in_=q_bf[:].rearrange("p m j -> p (m j)"))
 
         k_code = rows.tile([P, N], U32, name="k_code", align_bytes=64, offset=NQ)
-        acc = [psum.tile([P, N], F32, name=f"acc{t}") for t in range(QT)]
+        acc = [[psum.tile([P, HALF], F32, name=f"acc{t}_{h}") for h in range(2)] for t in range(QT)]
         for h in range(2):
             cols = slice(h * HALF, (h + 1) * HALF)
             listed = offsets[:, h * HALF // 16 : (h + 1) * HALF // 16]
             nc.vector.tensor_copy(k_code[:, cols], word_pool[:].bitcast(U32).indirect(listed))
             for t in range(QT):
                 nc.tensor.matmul_mx(
-                    out=acc[t][:, cols],
+                    out=acc[t][h][:],
                     lhsT=q_code[:, t * P : (t + 1) * P].bitcast(FP8X4),
                     lhsT_scale=q_scale[:, t * P : (t + 1) * P],
                     rhs=k_code[:, cols].bitcast(FP8X4),
@@ -128,17 +133,44 @@ def tile_attend_link_resid_topk_kernel(tc, qT, k_words, k_scales, kb, rt, ub, wt
         unbiased = [keep.tile([P, N], F32, name=f"unbiased{t}") for t in range(QT)]
         resid = [keep.tile([P, N], F32, name=f"resid{t}") for t in range(QT)]
         res = [keep.tile([P, N], F32, name=f"res{t}") for t in range(QT)]
-        for t in range(QT):
-            nc.vector.tensor_tensor(out=unbiased[t][:], in0=rt_sb[t][:], in1=kb_all[:], op=SUB)
-        for t in range(QT):
-            nc.vector.tensor_tensor(out=resid[t][:], in0=unbiased[t][:], in1=acc[t][:], op=SUB)
-        for t, cols in ((0, slice(0, N)), (1, slice(0, HALF)), (1, slice(HALF, N))):
+        halves = (slice(0, HALF), slice(HALF, N))
+
+        def less_kb(t, h):
+            cols = halves[h]
+            nc.vector.tensor_tensor(out=unbiased[t][:, cols], in0=rt_sb[t][:, cols], in1=kb_all[:, cols], op=SUB)
+
+        def less_scores(t, h):
+            cols = halves[h]
+            nc.vector.tensor_tensor(out=resid[t][:, cols], in0=unbiased[t][:, cols], in1=acc[t][h][:], op=SUB)
+
+        def store(t, h):
+            nc.sync.dma_start(out=out[0, t * P : (t + 1) * P, halves[h]], in_=res[t][:, halves[h]])
+
+        def weigh(t, h):
+            cols = halves[h]
             nc.vector.scalar_tensor_tensor(
                 out=res[t][:, cols],
                 in0=resid[t][:, cols],
-                scalar=ub_sb[:, t : t + 1],
+                scalar=ub_turned[:, t : t + 1],
                 in1=wt_sb[t][:, cols],
                 op0=SUB,
                 op1=MULT,
             )
-            nc.sync.dma_start(out=out[0, t * P : (t + 1) * P, cols], in_=res[t][:, cols])
+            store(t, h)
+
+        first = halves[0]
+        nc.gpsimd.tensor_tensor(out=unbiased[0][:, first], in0=rt_sb[0][:, first], in1=kb_sb[:], op=SUB)
+        less_kb(0, 1)
+        less_kb(1, 0)
+        nc.vector.scalar_tensor_tensor(
+            out=resid[0][:, first], in0=unbiased[0][:, first], scalar=ub_turned[:, 0:1], in1=acc[0][0][:], op0=SUB, op1=SUB
+        )
+        nc.gpsimd.tensor_tensor(out=res[0][:, first], in0=resid[0][:, first], in1=wt_sb[0][:, first], op=MULT)
+        store(0, 0)
+        less_kb(1, 1)
+        less_scores(0, 1)
+        less_scores(1, 0)
+        less_scores(1, 1)
+        weigh(0, 1)
+        weigh(1, 0)
+        weigh(1, 1)

@@ -12,6 +12,7 @@ U8 = mybir.dt.uint8
 FP8X4 = mybir.dt.float8_e4m3fn_x4
 SUB = mybir.AluOpType.subtract
 MULT = mybir.AluOpType.mult
+IDENTITY = mybir.ActivationFunctionType.Identity
 
 P = 128
 PACK = 4
@@ -115,20 +116,39 @@ def tile_attend_link_resid_topk_kernel(tc, qT, k_words, k_scales, kb, rt, ub, wt
 
         k_code = rows.tile([P, N], U32, name="k_code", align_bytes=64, offset=NQ)
         acc = [[psum.tile([P, HALF], F32, name=f"acc{t}_{h}") for h in range(2)] for t in range(QT)]
-        for h in range(2):
-            cols = slice(h * HALF, (h + 1) * HALF)
+
+        def product(dst, left, left_scale, right, right_scale):
+            nc.tensor.matmul_mx(
+                out=dst,
+                lhsT=left.bitcast(FP8X4),
+                lhsT_scale=left_scale,
+                rhs=right.bitcast(FP8X4),
+                rhs_scale=right_scale,
+                start=True,
+                stop=True,
+            )
+
+        def gather_words(h):
             listed = offsets[:, h * HALF // 16 : (h + 1) * HALF // 16]
-            nc.vector.tensor_copy(k_code[:, cols], word_pool[:].bitcast(U32).indirect(listed))
-            for t in range(QT):
-                nc.tensor.matmul_mx(
-                    out=acc[t][h][:],
-                    lhsT=q_code[:, t * P : (t + 1) * P].bitcast(FP8X4),
-                    lhsT_scale=q_scale[:, t * P : (t + 1) * P],
-                    rhs=k_code[:, cols].bitcast(FP8X4),
-                    rhs_scale=k_scale[:, cols],
-                    start=True,
-                    stop=True,
-                )
+            nc.vector.tensor_copy(k_code[:, h * HALF : (h + 1) * HALF], word_pool[:].bitcast(U32).indirect(listed))
+
+        def score(t, h):
+            cols, queries = slice(h * HALF, (h + 1) * HALF), slice(t * P, (t + 1) * P)
+            product(acc[t][h][:], q_code[:, queries], q_scale[:, queries], k_code[:, cols], k_scale[:, cols])
+
+        gather_words(0)
+        score(0, 0)
+        by_slot = [keep.tile([P, P], F32, name=f"by_slot{c}") for c in range(CH // 2)]
+        for c in range(CH // 2):
+            slots = slice(c * P, (c + 1) * P)
+            acc_slot = psum.tile([P, P], F32, name=f"acc_slot{c}")
+            product(acc_slot[:], k_code[:, slots], k_scale[:, slots], q_code[:, P:], q_scale[:, P:])
+            nc.scalar.activation(out=by_slot[c][:], in_=acc_slot[:], func=IDENTITY, bias=kb_col[:, c : c + 1])
+        gather_words(1)
+        score(0, 1)
+        score(1, 1)
+        for c in range(CH // 2):
+            nc.tensor.transpose(acc[1][0][:, c * P : (c + 1) * P], by_slot[c][:], ident[:])
 
         unbiased = [keep.tile([P, N], F32, name=f"unbiased{t}") for t in range(QT)]
         resid = [keep.tile([P, N], F32, name=f"resid{t}") for t in range(QT)]
@@ -161,16 +181,15 @@ def tile_attend_link_resid_topk_kernel(tc, qT, k_words, k_scales, kb, rt, ub, wt
         first = halves[0]
         nc.gpsimd.tensor_tensor(out=unbiased[0][:, first], in0=rt_sb[0][:, first], in1=kb_sb[:], op=SUB)
         less_kb(0, 1)
-        less_kb(1, 0)
+        less_kb(1, 1)
         nc.vector.scalar_tensor_tensor(
             out=resid[0][:, first], in0=unbiased[0][:, first], scalar=ub_turned[:, 0:1], in1=acc[0][0][:], op0=SUB, op1=SUB
         )
         nc.gpsimd.tensor_tensor(out=res[0][:, first], in0=resid[0][:, first], in1=wt_sb[0][:, first], op=MULT)
         store(0, 0)
-        less_kb(1, 1)
         less_scores(0, 1)
-        less_scores(1, 0)
         less_scores(1, 1)
+        nc.vector.tensor_tensor(out=resid[1][:, first], in0=rt_sb[1][:, first], in1=acc[1][0][:], op=SUB)
         weigh(0, 1)
-        weigh(1, 0)
         weigh(1, 1)
+        weigh(1, 0)

@@ -25,7 +25,8 @@ QUAD = 32
 CH = N // P
 HALF = N // 2
 KB_ROW = P - 1
-KB_POOL_COLS = 1368
+KB_POOL_COLS = 1320
+SCALE_POOL_WORDS = T // 8
 LATE_WORDS = T + 2 * QT * N
 
 FLOPS = 2 * D * NQ * N
@@ -46,6 +47,9 @@ def tile_attend_link_resid_topk_kernel(tc, qT, k_words, k_scales, kb, rt, ub, wt
         kb_pool = window.tile([P, T + 1], F32, name="kb_pool", align_bytes=64, offset=0)
         nc.scalar.dma_start(out=kb_pool[KB_ROW:P, :T], in_=kb[0:1, :])
 
+        scale_pool = keep.tile([P, T + 4], U8, name="scale_pool", align_bytes=64)
+        scale_words = scale_pool[:].bitcast(I32)
+        nc.gpsimd.memset(scale_words[:, :SCALE_POOL_WORDS], 0)
         nc.gpsimd.memset(kb_pool[0:KB_ROW, :KB_POOL_COLS].bitcast(I32), 0)
 
         q_raw = keep.tile([P, PACK, NQ], F32, name="q_raw")
@@ -58,8 +62,7 @@ def tile_attend_link_resid_topk_kernel(tc, qT, k_words, k_scales, kb, rt, ub, wt
 
         zeros = late.tile([P, LATE_WORDS], F32, name="zeros", align_bytes=64, offset=0)
         nc.vector.memset(zeros[:, : P + 1], 0.0)
-        scale_pool = keep.tile([P, T + 4], U8, name="scale_pool", align_bytes=64)
-        nc.vector.memset(scale_pool[:].bitcast(I32), 0)
+        nc.vector.memset(scale_words[:, SCALE_POOL_WORDS:], 0)
         for quad in range(P // QUAD):
             nc.sync.dma_start(
                 out=scale_pool[QUAD * quad : QUAD * quad + PACK, :T].bitcast(I32),
@@ -100,13 +103,13 @@ def tile_attend_link_resid_topk_kernel(tc, qT, k_words, k_scales, kb, rt, ub, wt
         turned = psum.tile([P, CH, P], F32, name="turned")
         for c in range(CH):
             nc.tensor.transpose(turned[:, c, :], kb_row[:, c * P : (c + 1) * P], ident[:])
-        nc.vector.tensor_copy(kb_col[:], turned[:, :, KB_ROW])
+        nc.scalar.copy(out=kb_col[:], in_=turned[:, :, KB_ROW])
         kb_all = psum.tile([P, N], F32, name="kb_all")
         for c in range(CH):
             nc.tensor.transpose(kb_all[:, c * P : (c + 1) * P], kb_col[:, c : c + 1].to_broadcast([P, P]), ident[:])
 
         kb_sb = keep.tile([P, HALF], F32, name="kb_sb")
-        nc.scalar.copy(out=kb_sb[:], in_=kb_all[:, :HALF])
+        nc.scalar.copy(out=kb_sb[:], in_=kb_all[:, HALF:])
         ub_turned = psum.tile([P, CH, P], F32, name="ub_turned", tag="turned")[:, 0, :]
         nc.tensor.transpose(ub_turned, ub_rows[:], ident[:])
 
@@ -145,8 +148,8 @@ def tile_attend_link_resid_topk_kernel(tc, qT, k_words, k_scales, kb, rt, ub, wt
             product(acc_slot[:], k_code[:, slots], k_scale[:, slots], q_code[:, P:], q_scale[:, P:])
             nc.scalar.activation(out=by_slot[c][:], in_=acc_slot[:], func=IDENTITY, bias=kb_col[:, c : c + 1])
         gather_words(1)
-        score(0, 1)
         score(1, 1)
+        score(0, 1)
         for c in range(CH // 2):
             nc.tensor.transpose(acc[1][0][:, c * P : (c + 1) * P], by_slot[c][:], ident[:])
 
@@ -178,17 +181,17 @@ def tile_attend_link_resid_topk_kernel(tc, qT, k_words, k_scales, kb, rt, ub, wt
             )
             store(t, h)
 
-        first = halves[0]
-        nc.gpsimd.tensor_tensor(out=unbiased[0][:, first], in0=rt_sb[0][:, first], in1=kb_sb[:], op=SUB)
-        less_kb(0, 1)
+        first, second = halves
+        nc.gpsimd.tensor_tensor(out=unbiased[0][:, second], in0=rt_sb[0][:, second], in1=kb_sb[:], op=SUB)
+        less_kb(0, 0)
         less_kb(1, 1)
         nc.vector.scalar_tensor_tensor(
             out=resid[0][:, first], in0=unbiased[0][:, first], scalar=ub_turned[:, 0:1], in1=acc[0][0][:], op0=SUB, op1=SUB
         )
         nc.gpsimd.tensor_tensor(out=res[0][:, first], in0=resid[0][:, first], in1=wt_sb[0][:, first], op=MULT)
         store(0, 0)
-        less_scores(0, 1)
         less_scores(1, 1)
+        less_scores(0, 1)
         nc.vector.tensor_tensor(out=resid[1][:, first], in0=rt_sb[1][:, first], in1=acc[1][0][:], op=SUB)
         weigh(0, 1)
         weigh(1, 1)

@@ -25,9 +25,10 @@ QUAD = 32
 CH = N // P
 HALF = N // 2
 KB_ROW = P - 1
-KB_POOL_COLS = 1320
-SCALE_POOL_WORDS = T // 8
-LATE_WORDS = T + 2 * QT * N
+UB_ROW = P - QT
+KB_POOL_COLS = 1176
+SCALE_ROWS = 16
+SCALE_FROM = 48
 
 FLOPS = 2 * D * NQ * N
 BYTES = 4 * D * NQ + D * T + (D // 32) * T + 4 * T + 3 * 4 * NQ * N + 4 * NQ + 2 * P * (N // 16)
@@ -37,87 +38,94 @@ def tile_attend_link_resid_topk_kernel(tc, qT, k_words, k_scales, kb, rt, ub, wt
     nc = tc.nc
     with ExitStack() as ctx:
         keep = ctx.enter_context(tc.tile_pool(name="keep", bufs=1))
-        late = ctx.enter_context(tc.tile_pool(name="late", bufs=1))
         window = ctx.enter_context(tc.tile_pool(name="window", bufs=1))
         rows = ctx.enter_context(tc.tile_pool(name="rows", bufs=1))
         psum = ctx.enter_context(tc.psum_pool(name="psum", bufs=1))
 
         offsets = keep.tile([P, N // 16], U16, name="offsets")
         nc.sync.dma_start(offsets[:], offs)
+        scale_pool = rows.tile([P, T + 4], U8, name="scale_pool", align_bytes=64, offset=T)
+        scale_words = scale_pool[:].bitcast(I32)
+        nc.scalar.dma_start(
+            out=scale_pool[SCALE_FROM : SCALE_FROM + SCALE_ROWS, :T].bitcast(I32), in_=k_scales[0].bitcast(I32)
+        )
         kb_pool = window.tile([P, T + 1], F32, name="kb_pool", align_bytes=64, offset=0)
         nc.scalar.dma_start(out=kb_pool[KB_ROW:P, :T], in_=kb[0:1, :])
-
-        scale_pool = keep.tile([P, T + 4], U8, name="scale_pool", align_bytes=64)
-        scale_words = scale_pool[:].bitcast(I32)
-        nc.gpsimd.memset(scale_words[:, :SCALE_POOL_WORDS], 0)
-        nc.gpsimd.memset(kb_pool[0:KB_ROW, :KB_POOL_COLS].bitcast(I32), 0)
-
-        q_raw = keep.tile([P, PACK, NQ], F32, name="q_raw")
-        nc.scalar.dma_start(out=q_raw[:], in_=qT[0].rearrange("(p j) w -> p j w", j=PACK))
-
-        warm_in = keep.tile([P, 1], F32, name="warm_in")
-        nc.vector.memset(warm_in[:], 0.0)
-        warm_out = keep.tile([P, 1], F32, name="warm_out")
-        nc.scalar.copy(out=warm_out[:], in_=warm_in[:])
-
-        zeros = late.tile([P, LATE_WORDS], F32, name="zeros", align_bytes=64, offset=0)
-        nc.vector.memset(zeros[:, : P + 1], 0.0)
-        nc.vector.memset(scale_words[:, SCALE_POOL_WORDS:], 0)
-        for quad in range(P // QUAD):
-            nc.sync.dma_start(
-                out=scale_pool[QUAD * quad : QUAD * quad + PACK, :T].bitcast(I32),
-                in_=k_scales[0, PACK * quad : PACK * (quad + 1), :].bitcast(I32),
-            )
-
-        ident = keep.tile([P, P], F32, name="ident")
-        nc.vector.tensor_tensor(out=ident[:], in0=zeros[:, :P], in1=zeros[:, 1 : P + 1], op=SUB)
-        make_identity(nc, ident[:], nomemset=True)
+        q_raw = window.tile([P, PACK, NQ], F32, name="q_raw", align_bytes=64, offset=8 * T)
+        nc.sync.dma_start(out=q_raw[:], in_=qT[0].rearrange("(p j) w -> p j w", j=PACK))
         ub_rows = keep.tile([P, P], F32, name="ub_rows")
-        nc.vector.tensor_tensor(out=ub_rows[:], in0=zeros[:, :P], in1=zeros[:, 1 : P + 1], op=SUB)
-        nc.vector.memset(kb_pool[0:KB_ROW, KB_POOL_COLS : T + 1].bitcast(I32), 0)
-
-        word_pool = late.tile([P, T], I32, name="word_pool", align_bytes=64, offset=0)
+        nc.sync.dma_start(out=ub_rows[UB_ROW:P, :], in_=ub[0].rearrange("(t p) o -> t (p o)", t=QT))
+        word_pool = keep.tile([P, T], I32, name="word_pool", align_bytes=64)
         nc.sync.dma_start(out=word_pool[:], in_=k_words[0].rearrange("p n r -> p (n r)").bitcast(I32))
-        nc.sync.dma_start(out=ub_rows[0:QT, :], in_=ub[0].rearrange("(t p) o -> t (p o)", t=QT))
-        rt_sb = [late.tile([P, N], F32, name=f"rt_sb{t}", align_bytes=64, offset=4 * (T + t * N)) for t in range(QT)]
+        rt_sb = [keep.tile([P, N], F32, name=f"rt_sb{t}") for t in range(QT)]
         wt_sb = [
-            late.tile([P, N], F32, name=f"wt_sb{t}", align_bytes=64, offset=4 * (T + (QT + t) * N)) for t in range(QT)
+            keep.tile([P, N], F32, name="wt_sb0"),
+            window.tile([P, N], F32, name="wt_sb1", align_bytes=64, offset=8 * T),
         ]
         for t in range(QT):
             nc.sync.dma_start(out=rt_sb[t][:], in_=rt[0, t * P : (t + 1) * P, :])
-        for t in range(QT):
-            nc.sync.dma_start(out=wt_sb[t][:], in_=wt[0, t * P : (t + 1) * P, :])
+        nc.sync.dma_start(out=wt_sb[0][:], in_=wt[0, :P, :])
 
+        nc.gpsimd.memset(scale_words[0:SCALE_FROM, :], 0)
+        nc.gpsimd.memset(kb_pool[0:KB_ROW, :KB_POOL_COLS].bitcast(I32), 0)
+
+        zero_col = keep.tile([P, 1], F32, name="zero_col")
+        nc.vector.memset(zero_col[:], 0.0)
+        nc.scalar.copy(out=ub_rows[0:UB_ROW, :], in_=zero_col[0:UB_ROW, :].to_broadcast([UB_ROW, P]))
+
+        nc.vector.memset(scale_words[SCALE_FROM + SCALE_ROWS :, :], 0)
+        ident_tile = keep.tile([P, P + 1], F32, name="ident_tile")
+        nc.vector.memset(ident_tile[:], 0.0)
+        ident = ident_tile[:, :P]
+        make_identity(nc, ident, nomemset=True)
+        nc.vector.memset(kb_pool[0:KB_ROW, KB_POOL_COLS : T + 1].bitcast(I32), 0)
+
+        k_scale = keep.tile([P, N + 4], U8, name="k_scale", align_bytes=64)
+        nc.vector.memset(k_scale[:].bitcast(I32), 0)
+        scale_rows = keep.tile([P, N], U8, name="scale_rows", align_bytes=64)
+        nc.vector.tensor_copy(scale_rows[:], scale_pool[:, :T].indirect(offsets[:]))
+        for quad in range(P // QUAD):
+            src = SCALE_FROM + quad * PACK
+            nc.scalar.dma_start(
+                out=k_scale[QUAD * quad : QUAD * quad + PACK, :N].bitcast(I32),
+                in_=scale_rows[src : src + PACK, :].bitcast(I32),
+            )
         kb_row = rows.tile([P, N], F32, name="kb_row", align_bytes=64, offset=64)
         nc.vector.tensor_copy(kb_row[:], kb_pool[:, :T].indirect(offsets[:]))
-        k_scale = window.tile([P, N], U8, name="k_scale", align_bytes=64, offset=4 * (NQ + N))
-        nc.vector.tensor_copy(k_scale[:], scale_pool[:, :T].indirect(offsets[:]))
 
-        q_bf = keep.tile([P, NQ, PACK], BF16, name="q_bf", align_bytes=64)
-        nc.scalar.copy(
-            out=q_bf[:].rearrange("p (c i) j -> p c j i", i=PACK),
-            in_=q_raw[:].rearrange("p j (c i) -> p c j i", i=PACK),
-        )
+        q_bf = [
+            window.tile([P, P, PACK], BF16, name="q_bf0", align_bytes=64, offset=4 * NQ),
+            rows.tile([P, P, PACK], BF16, name="q_bf1", align_bytes=64, offset=2 * T - 64),
+        ]
+        for t, cast in enumerate((nc.vector.tensor_copy, nc.scalar.copy)):
+            cast(
+                q_bf[t][:].rearrange("p (c i) j -> p c j i", i=PACK),
+                q_raw[:, :, t * P : (t + 1) * P].rearrange("p j (c i) -> p c j i", i=PACK),
+            )
+        nc.sync.dma_start(out=wt_sb[1][:], in_=wt[0, P:, :])
 
         kb_col = keep.tile([P, CH], F32, name="kb_col")
         turned = psum.tile([P, CH, P], F32, name="turned")
         for c in range(CH):
-            nc.tensor.transpose(turned[:, c, :], kb_row[:, c * P : (c + 1) * P], ident[:])
+            nc.tensor.transpose(turned[:, c, :], kb_row[:, c * P : (c + 1) * P], ident)
         nc.scalar.copy(out=kb_col[:], in_=turned[:, :, KB_ROW])
         kb_all = psum.tile([P, N], F32, name="kb_all")
         for c in range(CH):
-            nc.tensor.transpose(kb_all[:, c * P : (c + 1) * P], kb_col[:, c : c + 1].to_broadcast([P, P]), ident[:])
+            nc.tensor.transpose(kb_all[:, c * P : (c + 1) * P], kb_col[:, c : c + 1].to_broadcast([P, P]), ident)
 
         kb_sb = keep.tile([P, HALF], F32, name="kb_sb")
         nc.scalar.copy(out=kb_sb[:], in_=kb_all[:, HALF:])
         ub_turned = psum.tile([P, CH, P], F32, name="ub_turned", tag="turned")[:, 0, :]
-        nc.tensor.transpose(ub_turned, ub_rows[:], ident[:])
+        nc.tensor.transpose(ub_turned, ub_rows[:], ident)
 
-        q_code = window.tile([P, NQ], U32, name="q_code", align_bytes=64, offset=0)
-        q_scale = rows.tile([P, NQ], U8, name="q_scale", align_bytes=64, offset=0)
-        nc.vector.quantize_mx(out=q_code[:].bitcast(FP8X4), scales=q_scale[:], in_=q_bf[:].rearrange("p m j -> p (m j)"))
+        q_code = [window.tile([P, P], U32, name=f"q_code{t}", align_bytes=64, offset=4 * P * t) for t in range(QT)]
+        q_scale = [keep.tile([P, P], U8, name=f"q_scale{t}", align_bytes=64) for t in range(QT)]
+        for t in (1, 0):
+            nc.vector.quantize_mx(
+                out=q_code[t][:].bitcast(FP8X4), scales=q_scale[t][:], in_=q_bf[t][:].rearrange("p m j -> p (m j)")
+            )
 
-        k_code = rows.tile([P, N], U32, name="k_code", align_bytes=64, offset=NQ)
+        k_code = rows.tile([P, N], U32, name="k_code", align_bytes=64, offset=T)
         acc = [[psum.tile([P, HALF], F32, name=f"acc{t}_{h}") for h in range(2)] for t in range(QT)]
 
         def product(dst, left, left_scale, right, right_scale):
@@ -136,8 +144,8 @@ def tile_attend_link_resid_topk_kernel(tc, qT, k_words, k_scales, kb, rt, ub, wt
             nc.vector.tensor_copy(k_code[:, h * HALF : (h + 1) * HALF], word_pool[:].bitcast(U32).indirect(listed))
 
         def score(t, h):
-            cols, queries = slice(h * HALF, (h + 1) * HALF), slice(t * P, (t + 1) * P)
-            product(acc[t][h][:], q_code[:, queries], q_scale[:, queries], k_code[:, cols], k_scale[:, cols])
+            cols = slice(h * HALF, (h + 1) * HALF)
+            product(acc[t][h][:], q_code[t][:], q_scale[t][:], k_code[:, cols], k_scale[:, cols])
 
         gather_words(0)
         score(0, 0)
@@ -145,13 +153,13 @@ def tile_attend_link_resid_topk_kernel(tc, qT, k_words, k_scales, kb, rt, ub, wt
         for c in range(CH // 2):
             slots = slice(c * P, (c + 1) * P)
             acc_slot = psum.tile([P, P], F32, name=f"acc_slot{c}")
-            product(acc_slot[:], k_code[:, slots], k_scale[:, slots], q_code[:, P:], q_scale[:, P:])
+            product(acc_slot[:], k_code[:, slots], k_scale[:, slots], q_code[1][:], q_scale[1][:])
             nc.scalar.activation(out=by_slot[c][:], in_=acc_slot[:], func=IDENTITY, bias=kb_col[:, c : c + 1])
         gather_words(1)
         score(1, 1)
         score(0, 1)
         for c in range(CH // 2):
-            nc.tensor.transpose(acc[1][0][:, c * P : (c + 1) * P], by_slot[c][:], ident[:])
+            nc.tensor.transpose(acc[1][0][:, c * P : (c + 1) * P], by_slot[c][:], ident)
 
         unbiased = [keep.tile([P, N], F32, name=f"unbiased{t}") for t in range(QT)]
         resid = [keep.tile([P, N], F32, name=f"resid{t}") for t in range(QT)]
@@ -174,7 +182,7 @@ def tile_attend_link_resid_topk_kernel(tc, qT, k_words, k_scales, kb, rt, ub, wt
             nc.vector.scalar_tensor_tensor(
                 out=res[t][:, cols],
                 in0=resid[t][:, cols],
-                scalar=ub_turned[:, t : t + 1],
+                scalar=ub_turned[:, UB_ROW + t : UB_ROW + t + 1],
                 in1=wt_sb[t][:, cols],
                 op0=SUB,
                 op1=MULT,
@@ -186,7 +194,7 @@ def tile_attend_link_resid_topk_kernel(tc, qT, k_words, k_scales, kb, rt, ub, wt
         less_kb(0, 0)
         less_kb(1, 1)
         nc.vector.scalar_tensor_tensor(
-            out=resid[0][:, first], in0=unbiased[0][:, first], scalar=ub_turned[:, 0:1], in1=acc[0][0][:], op0=SUB, op1=SUB
+            out=resid[0][:, first], in0=unbiased[0][:, first], scalar=ub_turned[:, UB_ROW : UB_ROW + 1], in1=acc[0][0][:], op0=SUB, op1=SUB
         )
         nc.gpsimd.tensor_tensor(out=res[0][:, first], in0=resid[0][:, first], in1=wt_sb[0][:, first], op=MULT)
         store(0, 0)

@@ -26,7 +26,6 @@ CH = N // P
 HALF = N // 2
 KB_ROW = P - 1
 UB_ROW = P - QT
-KB_POOL_COLS = 1176
 SCALE_ROWS = 16
 SCALE_FROM = 48
 
@@ -44,7 +43,7 @@ def tile_attend_link_resid_topk_kernel(tc, qT, k_words, k_scales, kb, rt, ub, wt
 
         offsets = keep.tile([P, N // 16], U16, name="offsets")
         nc.sync.dma_start(offsets[:], offs)
-        scale_pool = rows.tile([P, T + 4], U8, name="scale_pool", align_bytes=64, offset=T)
+        scale_pool = rows.tile([P, T + 4], U8, name="scale_pool", align_bytes=64, offset=960)
         scale_words = scale_pool[:].bitcast(I32)
         nc.scalar.dma_start(
             out=scale_pool[SCALE_FROM : SCALE_FROM + SCALE_ROWS, :T].bitcast(I32), in_=k_scales[0].bitcast(I32)
@@ -66,19 +65,18 @@ def tile_attend_link_resid_topk_kernel(tc, qT, k_words, k_scales, kb, rt, ub, wt
             nc.sync.dma_start(out=rt_sb[t][:], in_=rt[0, t * P : (t + 1) * P, :])
         nc.sync.dma_start(out=wt_sb[0][:], in_=wt[0, :P, :])
 
-        nc.gpsimd.memset(scale_words[0:SCALE_FROM, :], 0)
-        nc.gpsimd.memset(kb_pool[0:KB_ROW, :KB_POOL_COLS].bitcast(I32), 0)
+        nc.gpsimd.memset(kb_pool[0:KB_ROW, :].bitcast(I32), 0)
 
         zero_col = keep.tile([P, 1], F32, name="zero_col")
         nc.vector.memset(zero_col[:], 0.0)
         nc.scalar.copy(out=ub_rows[0:UB_ROW, :], in_=zero_col[0:UB_ROW, :].to_broadcast([UB_ROW, P]))
 
+        nc.vector.memset(scale_words[0:SCALE_FROM, :], 0)
         nc.vector.memset(scale_words[SCALE_FROM + SCALE_ROWS :, :], 0)
         ident_tile = keep.tile([P, P + 1], F32, name="ident_tile")
         nc.vector.memset(ident_tile[:], 0.0)
         ident = ident_tile[:, :P]
         make_identity(nc, ident, nomemset=True)
-        nc.vector.memset(kb_pool[0:KB_ROW, KB_POOL_COLS : T + 1].bitcast(I32), 0)
 
         k_scale = keep.tile([P, N + 4], U8, name="k_scale", align_bytes=64)
         nc.vector.memset(k_scale[:].bitcast(I32), 0)
@@ -90,12 +88,17 @@ def tile_attend_link_resid_topk_kernel(tc, qT, k_words, k_scales, kb, rt, ub, wt
                 out=k_scale[QUAD * quad : QUAD * quad + PACK, :N].bitcast(I32),
                 in_=scale_rows[src : src + PACK, :].bitcast(I32),
             )
-        kb_row = rows.tile([P, N], F32, name="kb_row", align_bytes=64, offset=64)
-        nc.vector.tensor_copy(kb_row[:], kb_pool[:, :T].indirect(offsets[:]))
+        listed = [offsets[:, h * HALF // 16 : (h + 1) * HALF // 16] for h in range(2)]
+        kb_row = [
+            rows.tile([P, HALF], F32, name="kb_row0", align_bytes=64, offset=1024),
+            rows.tile([P, HALF], F32, name="kb_row1", align_bytes=64, offset=2048),
+        ]
+        for h in (1, 0):
+            nc.vector.tensor_copy(kb_row[h][:], kb_pool[:, :T].indirect(listed[h]))
 
         q_bf = [
             window.tile([P, P, PACK], BF16, name="q_bf0", align_bytes=64, offset=4 * NQ),
-            rows.tile([P, P, PACK], BF16, name="q_bf1", align_bytes=64, offset=2 * T - 64),
+            rows.tile([P, P, PACK], BF16, name="q_bf1", align_bytes=64, offset=0),
         ]
         for t, cast in enumerate((nc.vector.tensor_copy, nc.scalar.copy)):
             cast(
@@ -104,19 +107,15 @@ def tile_attend_link_resid_topk_kernel(tc, qT, k_words, k_scales, kb, rt, ub, wt
             )
         nc.sync.dma_start(out=wt_sb[1][:], in_=wt[0, P:, :])
 
-        kb_col = keep.tile([P, CH], F32, name="kb_col")
-        turned = psum.tile([P, CH, P], F32, name="turned")
-        for c in range(CH):
-            nc.tensor.transpose(turned[:, c, :], kb_row[:, c * P : (c + 1) * P], ident)
-        nc.scalar.copy(out=kb_col[:], in_=turned[:, :, KB_ROW])
-        kb_all = psum.tile([P, N], F32, name="kb_all")
-        for c in range(CH):
-            nc.tensor.transpose(kb_all[:, c * P : (c + 1) * P], kb_col[:, c : c + 1].to_broadcast([P, P]), ident)
-
-        kb_sb = keep.tile([P, HALF], F32, name="kb_sb")
-        nc.scalar.copy(out=kb_sb[:], in_=kb_all[:, HALF:])
-        ub_turned = psum.tile([P, CH, P], F32, name="ub_turned", tag="turned")[:, 0, :]
+        kb_and_ub = psum.tile([P, HALF + P], F32, name="kb_and_ub")
+        ub_turned = kb_and_ub[:, HALF:]
         nc.tensor.transpose(ub_turned, ub_rows[:], ident)
+        kb_second = psum.tile([P, HALF], F32, name="kb_second")
+        kb_all = [kb_and_ub[:, :HALF], kb_second[:]]
+        turned = [psum.tile([P, CH // 2, P], F32, name=f"turned{h}") for h in range(2)]
+        for h in (1, 0):
+            for c in range(CH // 2):
+                nc.tensor.transpose(turned[h][:, c, :], kb_row[h][:, c * P : (c + 1) * P], ident)
 
         q_code = [window.tile([P, P], U32, name=f"q_code{t}", align_bytes=64, offset=4 * P * t) for t in range(QT)]
         q_scale = [keep.tile([P, P], U8, name=f"q_scale{t}", align_bytes=64) for t in range(QT)]
@@ -125,8 +124,26 @@ def tile_attend_link_resid_topk_kernel(tc, qT, k_words, k_scales, kb, rt, ub, wt
                 out=q_code[t][:].bitcast(FP8X4), scales=q_scale[t][:], in_=q_bf[t][:].rearrange("p m j -> p (m j)")
             )
 
-        k_code = rows.tile([P, N], U32, name="k_code", align_bytes=64, offset=T)
-        acc = [[psum.tile([P, HALF], F32, name=f"acc{t}_{h}") for h in range(2)] for t in range(QT)]
+        kb_col = [
+            keep.tile([P, CH // 2], F32, name="kb_col0"),
+            rows.tile([P, CH // 2], F32, name="kb_col1", align_bytes=64, offset=0),
+        ]
+        for h in (1, 0):
+            nc.vector.tensor_copy(kb_col[h][:], turned[h][:, :, KB_ROW])
+        for h in (1, 0):
+            for c in range(CH // 2):
+                nc.tensor.transpose(
+                    kb_all[h][:, c * P : (c + 1) * P], kb_col[h][:, c : c + 1].to_broadcast([P, P]), ident
+                )
+
+        kb_sb = keep.tile([P, HALF], F32, name="kb_sb")
+        nc.scalar.copy(out=kb_sb[:], in_=kb_all[1])
+
+        k_code = rows.tile([P, N], U32, name="k_code", align_bytes=64, offset=512)
+        acc = [
+            [psum.tile([P, HALF], F32, name="acc0_0", tag="turned0"), psum.tile([P, HALF], F32, name="acc0_1")],
+            [psum.tile([P, HALF], F32, name="acc1_0"), psum.tile([P, HALF], F32, name="acc1_1")],
+        ]
 
         def product(dst, left, left_scale, right, right_scale):
             nc.tensor.matmul_mx(
@@ -140,8 +157,7 @@ def tile_attend_link_resid_topk_kernel(tc, qT, k_words, k_scales, kb, rt, ub, wt
             )
 
         def gather_words(h):
-            listed = offsets[:, h * HALF // 16 : (h + 1) * HALF // 16]
-            nc.vector.tensor_copy(k_code[:, h * HALF : (h + 1) * HALF], word_pool[:].bitcast(U32).indirect(listed))
+            nc.vector.tensor_copy(k_code[:, h * HALF : (h + 1) * HALF], word_pool[:].bitcast(U32).indirect(listed[h]))
 
         def score(t, h):
             cols = slice(h * HALF, (h + 1) * HALF)
@@ -152,9 +168,9 @@ def tile_attend_link_resid_topk_kernel(tc, qT, k_words, k_scales, kb, rt, ub, wt
         by_slot = [keep.tile([P, P], F32, name=f"by_slot{c}") for c in range(CH // 2)]
         for c in range(CH // 2):
             slots = slice(c * P, (c + 1) * P)
-            acc_slot = psum.tile([P, P], F32, name=f"acc_slot{c}")
+            acc_slot = psum.tile([P, P], F32, name=f"acc_slot{c}", tag=("turned1", "acc_slot1")[c])
             product(acc_slot[:], k_code[:, slots], k_scale[:, slots], q_code[1][:], q_scale[1][:])
-            nc.scalar.activation(out=by_slot[c][:], in_=acc_slot[:], func=IDENTITY, bias=kb_col[:, c : c + 1])
+            nc.scalar.activation(out=by_slot[c][:], in_=acc_slot[:], func=IDENTITY, bias=kb_col[0][:, c : c + 1])
         gather_words(1)
         score(1, 1)
         score(0, 1)
@@ -168,7 +184,7 @@ def tile_attend_link_resid_topk_kernel(tc, qT, k_words, k_scales, kb, rt, ub, wt
 
         def less_kb(t, h):
             cols = halves[h]
-            nc.vector.tensor_tensor(out=unbiased[t][:, cols], in0=rt_sb[t][:, cols], in1=kb_all[:, cols], op=SUB)
+            nc.vector.tensor_tensor(out=unbiased[t][:, cols], in0=rt_sb[t][:, cols], in1=kb_all[h], op=SUB)
 
         def less_scores(t, h):
             cols = halves[h]

@@ -43,7 +43,7 @@ def tile_attend_link_resid_topk_kernel(tc, qT, k_words, k_scales, kb, rt, ub, wt
 
         offsets = keep.tile([P, N // 16], U16, name="offsets")
         nc.sync.dma_start(offsets[:], offs)
-        scale_pool = rows.tile([P, T + 4], U8, name="scale_pool", align_bytes=64, offset=960)
+        scale_pool = rows.tile([P, T + 4], U8, name="scale_pool", align_bytes=64, offset=6080)
         scale_words = scale_pool[:].bitcast(I32)
         nc.scalar.dma_start(
             out=scale_pool[SCALE_FROM : SCALE_FROM + SCALE_ROWS, :T].bitcast(I32), in_=k_scales[0].bitcast(I32)
@@ -56,14 +56,8 @@ def tile_attend_link_resid_topk_kernel(tc, qT, k_words, k_scales, kb, rt, ub, wt
         nc.sync.dma_start(out=ub_rows[UB_ROW:P, :], in_=ub[0].rearrange("(t p) o -> t (p o)", t=QT))
         word_pool = keep.tile([P, T], I32, name="word_pool", align_bytes=64)
         nc.sync.dma_start(out=word_pool[:], in_=k_words[0].rearrange("p n r -> p (n r)").bitcast(I32))
-        rt_sb = [keep.tile([P, N], F32, name=f"rt_sb{t}") for t in range(QT)]
-        wt_sb = [
-            keep.tile([P, N], F32, name="wt_sb0"),
-            window.tile([P, N], F32, name="wt_sb1", align_bytes=64, offset=8 * T),
-        ]
-        for t in range(QT):
-            nc.sync.dma_start(out=rt_sb[t][:], in_=rt[0, t * P : (t + 1) * P, :])
-        nc.sync.dma_start(out=wt_sb[0][:], in_=wt[0, :P, :])
+        rt_first = keep.tile([P, N], F32, name="rt_first")
+        nc.sync.dma_start(out=rt_first[:], in_=rt[0, :P, :])
 
         nc.gpsimd.memset(kb_pool[0:KB_ROW, :].bitcast(I32), 0)
 
@@ -84,28 +78,31 @@ def tile_attend_link_resid_topk_kernel(tc, qT, k_words, k_scales, kb, rt, ub, wt
         nc.vector.tensor_copy(scale_rows[:], scale_pool[:, :T].indirect(offsets[:]))
         for quad in range(P // QUAD):
             src = SCALE_FROM + quad * PACK
-            nc.scalar.dma_start(
+            nc.sync.dma_start(
                 out=k_scale[QUAD * quad : QUAD * quad + PACK, :N].bitcast(I32),
                 in_=scale_rows[src : src + PACK, :].bitcast(I32),
             )
+        late = rows.tile([P, 3, N], F32, name="late", align_bytes=64, offset=0)
+        rt_sb = [rt_first[:], late[:, 0, :]]
+        wt_sb = [late[:, 1, :], late[:, 2, :]]
+        nc.sync.dma_start(out=rt_sb[1], in_=rt[0, P:, :])
+        for t in range(QT):
+            nc.sync.dma_start(out=wt_sb[t], in_=wt[0, t * P : (t + 1) * P, :])
         listed = [offsets[:, h * HALF // 16 : (h + 1) * HALF // 16] for h in range(2)]
-        kb_row = [
-            rows.tile([P, HALF], F32, name="kb_row0", align_bytes=64, offset=1024),
-            rows.tile([P, HALF], F32, name="kb_row1", align_bytes=64, offset=2048),
-        ]
+        kb_listed = rows.tile([P, N], F32, name="kb_listed", align_bytes=64, offset=8064)
+        kb_row = [kb_listed[:, :HALF], kb_listed[:, HALF:]]
         for h in (1, 0):
-            nc.vector.tensor_copy(kb_row[h][:], kb_pool[:, :T].indirect(listed[h]))
+            nc.vector.tensor_copy(kb_row[h], kb_pool[:, :T].indirect(listed[h]))
 
         q_bf = [
-            window.tile([P, P, PACK], BF16, name="q_bf0", align_bytes=64, offset=4 * NQ),
-            rows.tile([P, P, PACK], BF16, name="q_bf1", align_bytes=64, offset=0),
+            rows.tile([P, P, PACK], BF16, name="q_bf0", align_bytes=64, offset=11072),
+            keep.tile([P, P, PACK], BF16, name="q_bf1", align_bytes=64),
         ]
-        for t, cast in enumerate((nc.vector.tensor_copy, nc.scalar.copy)):
-            cast(
+        for t in (1, 0):
+            nc.scalar.copy(
                 q_bf[t][:].rearrange("p (c i) j -> p c j i", i=PACK),
                 q_raw[:, :, t * P : (t + 1) * P].rearrange("p j (c i) -> p c j i", i=PACK),
             )
-        nc.sync.dma_start(out=wt_sb[1][:], in_=wt[0, P:, :])
 
         kb_and_ub = psum.tile([P, HALF + P], F32, name="kb_and_ub")
         ub_turned = kb_and_ub[:, HALF:]
@@ -124,12 +121,9 @@ def tile_attend_link_resid_topk_kernel(tc, qT, k_words, k_scales, kb, rt, ub, wt
                 out=q_code[t][:].bitcast(FP8X4), scales=q_scale[t][:], in_=q_bf[t][:].rearrange("p m j -> p (m j)")
             )
 
-        kb_col = [
-            keep.tile([P, CH // 2], F32, name="kb_col0"),
-            rows.tile([P, CH // 2], F32, name="kb_col1", align_bytes=64, offset=0),
-        ]
+        kb_col = [keep.tile([P, CH // 2], F32, name=f"kb_col{h}") for h in range(2)]
         for h in (1, 0):
-            nc.vector.tensor_copy(kb_col[h][:], turned[h][:, :, KB_ROW])
+            nc.scalar.copy(out=kb_col[h][:], in_=turned[h][:, :, KB_ROW])
         for h in (1, 0):
             for c in range(CH // 2):
                 nc.tensor.transpose(
@@ -139,7 +133,7 @@ def tile_attend_link_resid_topk_kernel(tc, qT, k_words, k_scales, kb, rt, ub, wt
         kb_sb = keep.tile([P, HALF], F32, name="kb_sb")
         nc.scalar.copy(out=kb_sb[:], in_=kb_all[1])
 
-        k_code = rows.tile([P, N], U32, name="k_code", align_bytes=64, offset=512)
+        k_code = rows.tile([P, N], U32, name="k_code", align_bytes=64, offset=9088)
         acc = [
             [psum.tile([P, HALF], F32, name="acc0_0", tag="turned0"), psum.tile([P, HALF], F32, name="acc0_1")],
             [psum.tile([P, HALF], F32, name="acc1_0"), psum.tile([P, HALF], F32, name="acc1_1")],

@@ -13,6 +13,7 @@ FP8X4 = mybir.dt.float8_e4m3fn_x4
 SUB = mybir.AluOpType.subtract
 MULT = mybir.AluOpType.mult
 IDENTITY = mybir.ActivationFunctionType.Identity
+COPY = mybir.ActivationFunctionType.Copy
 
 P = 128
 PACK = 4
@@ -43,21 +44,19 @@ def tile_attend_link_resid_topk_kernel(tc, qT, k_words, k_scales, kb, rt, ub, wt
 
         offsets = keep.tile([P, N // 16], U16, name="offsets")
         nc.sync.dma_start(offsets[:], offs)
-        scale_pool = rows.tile([P, T + 4], U8, name="scale_pool", align_bytes=64, offset=6080)
+        scale_pool = rows.tile([P, T + 4], U8, name="scale_pool", align_bytes=64, offset=8128)
         scale_words = scale_pool[:].bitcast(I32)
         nc.scalar.dma_start(
             out=scale_pool[SCALE_FROM : SCALE_FROM + SCALE_ROWS, :T].bitcast(I32), in_=k_scales[0].bitcast(I32)
         )
-        kb_pool = window.tile([P, T + 1], F32, name="kb_pool", align_bytes=64, offset=0)
-        nc.scalar.dma_start(out=kb_pool[KB_ROW:P, :T], in_=kb[0:1, :])
+        kb_pool = keep.tile([P, T], F32, name="kb_pool", align_bytes=64)
+        nc.scalar.dma_start(out=kb_pool[KB_ROW:P, :], in_=kb[0:1, :])
         q_raw = window.tile([P, PACK, NQ], F32, name="q_raw", align_bytes=64, offset=8 * T)
         nc.sync.dma_start(out=q_raw[:], in_=qT[0].rearrange("(p j) w -> p j w", j=PACK))
         ub_rows = keep.tile([P, P], F32, name="ub_rows")
         nc.sync.dma_start(out=ub_rows[UB_ROW:P, :], in_=ub[0].rearrange("(t p) o -> t (p o)", t=QT))
         word_pool = keep.tile([P, T], I32, name="word_pool", align_bytes=64)
         nc.sync.dma_start(out=word_pool[:], in_=k_words[0].rearrange("p n r -> p (n r)").bitcast(I32))
-        rt_first = keep.tile([P, N], F32, name="rt_first")
-        nc.sync.dma_start(out=rt_first[:], in_=rt[0, :P, :])
 
         nc.gpsimd.memset(kb_pool[0:KB_ROW, :].bitcast(I32), 0)
 
@@ -82,24 +81,25 @@ def tile_attend_link_resid_topk_kernel(tc, qT, k_words, k_scales, kb, rt, ub, wt
                 out=k_scale[QUAD * quad : QUAD * quad + PACK, :N].bitcast(I32),
                 in_=scale_rows[src : src + PACK, :].bitcast(I32),
             )
-        late = rows.tile([P, 3, N], F32, name="late", align_bytes=64, offset=0)
-        rt_sb = [rt_first[:], late[:, 0, :]]
-        wt_sb = [late[:, 1, :], late[:, 2, :]]
-        nc.sync.dma_start(out=rt_sb[1], in_=rt[0, P:, :])
+        late = rows.tile([P, 4, N], F32, name="late", align_bytes=64, offset=0)
+        rt_sb = [late[:, 0, :], late[:, 1, :]]
+        wt_sb = [late[:, 2, :], late[:, 3, :]]
+        for t in range(QT):
+            nc.sync.dma_start(out=rt_sb[t], in_=rt[0, t * P : (t + 1) * P, :])
         for t in range(QT):
             nc.sync.dma_start(out=wt_sb[t], in_=wt[0, t * P : (t + 1) * P, :])
         listed = [offsets[:, h * HALF // 16 : (h + 1) * HALF // 16] for h in range(2)]
-        kb_listed = rows.tile([P, N], F32, name="kb_listed", align_bytes=64, offset=8064)
+        kb_listed = rows.tile([P, N], F32, name="kb_listed", align_bytes=64, offset=10240)
         kb_row = [kb_listed[:, :HALF], kb_listed[:, HALF:]]
         for h in (1, 0):
-            nc.vector.tensor_copy(kb_row[h], kb_pool[:, :T].indirect(listed[h]))
+            nc.scalar.activation(kb_row[h], kb_pool[:].indirect(listed[h]), COPY)
 
         q_bf = [
-            rows.tile([P, P, PACK], BF16, name="q_bf0", align_bytes=64, offset=11072),
+            rows.tile([P, P, PACK], BF16, name="q_bf0", align_bytes=64, offset=13248),
             keep.tile([P, P, PACK], BF16, name="q_bf1", align_bytes=64),
         ]
         for t in (1, 0):
-            nc.scalar.copy(
+            nc.vector.tensor_copy(
                 q_bf[t][:].rearrange("p (c i) j -> p c j i", i=PACK),
                 q_raw[:, :, t * P : (t + 1) * P].rearrange("p j (c i) -> p c j i", i=PACK),
             )
@@ -133,7 +133,7 @@ def tile_attend_link_resid_topk_kernel(tc, qT, k_words, k_scales, kb, rt, ub, wt
         kb_sb = keep.tile([P, HALF], F32, name="kb_sb")
         nc.scalar.copy(out=kb_sb[:], in_=kb_all[1])
 
-        k_code = rows.tile([P, N], U32, name="k_code", align_bytes=64, offset=9088)
+        k_code = rows.tile([P, N], U32, name="k_code", align_bytes=64, offset=11264)
         acc = [
             [psum.tile([P, HALF], F32, name="acc0_0", tag="turned0"), psum.tile([P, HALF], F32, name="acc0_1")],
             [psum.tile([P, HALF], F32, name="acc1_0"), psum.tile([P, HALF], F32, name="acc1_1")],

@@ -23,39 +23,45 @@ N = 512
 T = 2048
 QT = NQ // P
 QUAD = 32
-CH = N // P
 HALF = N // 2
+CHUNKS = HALF // P
+LIST_GROUP = 16
+ALIGN = 64
+
 KB_ROW = P - 1
 UB_ROW = P - QT
-SCALE_ROWS = 16
-SCALE_FROM = 48
+SCALE_ROWS = D // 32
+SCALE_FROM = P // 2 - SCALE_ROWS
+
+LATE_AT = 0
+SCALE_POOL_AT = LATE_AT + 4 * 2 * QT * N - ALIGN
+KB_LISTED_AT = SCALE_POOL_AT + T + ALIGN
+K_CODE_AT = KB_LISTED_AT + 4 * HALF
+Q_BF0_AT = K_CODE_AT + 4 * N - ALIGN
 
 FLOPS = 2 * D * NQ * N
-BYTES = 4 * D * NQ + D * T + (D // 32) * T + 4 * T + 3 * 4 * NQ * N + 4 * NQ + 2 * P * (N // 16)
+BYTES = 4 * D * NQ + D * T + SCALE_ROWS * T + 4 * T + 3 * 4 * NQ * N + 4 * NQ + 2 * P * (N // LIST_GROUP)
 
 
 def tile_attend_link_resid_topk_kernel(tc, qT, k_words, k_scales, kb, rt, ub, wt, offs, out):
     nc = tc.nc
     with ExitStack() as ctx:
         keep = ctx.enter_context(tc.tile_pool(name="keep", bufs=1))
-        window = ctx.enter_context(tc.tile_pool(name="window", bufs=1))
-        rows = ctx.enter_context(tc.tile_pool(name="rows", bufs=1))
+        shared = ctx.enter_context(tc.tile_pool(name="shared", bufs=1))
         psum = ctx.enter_context(tc.psum_pool(name="psum", bufs=1))
 
-        offsets = keep.tile([P, N // 16], U16, name="offsets")
+        offsets = keep.tile([P, N // LIST_GROUP], U16, name="offsets")
         nc.sync.dma_start(offsets[:], offs)
-        scale_pool = rows.tile([P, T + 4], U8, name="scale_pool", align_bytes=64, offset=8128)
+        scale_pool = shared.tile([P, T], U8, name="scale_pool", align_bytes=ALIGN, offset=SCALE_POOL_AT)
         scale_words = scale_pool[:].bitcast(I32)
-        nc.scalar.dma_start(
-            out=scale_pool[SCALE_FROM : SCALE_FROM + SCALE_ROWS, :T].bitcast(I32), in_=k_scales[0].bitcast(I32)
-        )
-        kb_pool = keep.tile([P, T], F32, name="kb_pool", align_bytes=64)
+        nc.scalar.dma_start(out=scale_words[SCALE_FROM : SCALE_FROM + SCALE_ROWS, :], in_=k_scales[0].bitcast(I32))
+        kb_pool = keep.tile([P, T], F32, name="kb_pool", align_bytes=ALIGN)
         nc.scalar.dma_start(out=kb_pool[KB_ROW:P, :], in_=kb[0:1, :])
-        q_raw = window.tile([P, PACK, NQ], F32, name="q_raw", align_bytes=64, offset=8 * T)
+        q_raw = keep.tile([P, PACK, NQ], F32, name="q_raw", align_bytes=ALIGN)
         nc.sync.dma_start(out=q_raw[:], in_=qT[0].rearrange("(p j) w -> p j w", j=PACK))
         ub_rows = keep.tile([P, P], F32, name="ub_rows")
         nc.sync.dma_start(out=ub_rows[UB_ROW:P, :], in_=ub[0].rearrange("(t p) o -> t (p o)", t=QT))
-        word_pool = keep.tile([P, T], I32, name="word_pool", align_bytes=64)
+        word_pool = keep.tile([P, T], I32, name="word_pool", align_bytes=ALIGN)
         nc.sync.dma_start(out=word_pool[:], in_=k_words[0].rearrange("p n r -> p (n r)").bitcast(I32))
 
         nc.gpsimd.memset(kb_pool[0:KB_ROW, :].bitcast(I32), 0)
@@ -64,39 +70,45 @@ def tile_attend_link_resid_topk_kernel(tc, qT, k_words, k_scales, kb, rt, ub, wt
         nc.vector.memset(zero_col[:], 0.0)
         nc.scalar.copy(out=ub_rows[0:UB_ROW, :], in_=zero_col[0:UB_ROW, :].to_broadcast([UB_ROW, P]))
 
-        nc.vector.memset(scale_words[0:SCALE_FROM, :], 0)
-        nc.vector.memset(scale_words[SCALE_FROM + SCALE_ROWS :, :], 0)
-        ident_tile = keep.tile([P, P + 1], F32, name="ident_tile")
-        nc.vector.memset(ident_tile[:], 0.0)
-        ident = ident_tile[:, :P]
-        make_identity(nc, ident, nomemset=True)
+        def zero_beside_gpsimd(words):
+            last = words.shape[1] - 1
+            nc.vector.memset(words[:, :last], 0)
+            nc.vector.memset(words[:, last:], 0)
 
-        k_scale = keep.tile([P, N + 4], U8, name="k_scale", align_bytes=64)
-        nc.vector.memset(k_scale[:].bitcast(I32), 0)
-        scale_rows = keep.tile([P, N], U8, name="scale_rows", align_bytes=64)
-        nc.vector.tensor_copy(scale_rows[:], scale_pool[:, :T].indirect(offsets[:]))
+        zero_beside_gpsimd(scale_words[0:SCALE_FROM, :])
+        zero_beside_gpsimd(scale_words[SCALE_FROM + SCALE_ROWS :, :])
+        ident = keep.tile([P, P], F32, name="ident")
+        zero_beside_gpsimd(ident[:])
+        make_identity(nc, ident[:], nomemset=True)
+
+        k_scale = keep.tile([P, N], U8, name="k_scale", align_bytes=ALIGN)
+        zero_beside_gpsimd(k_scale[:].bitcast(I32))
+        scale_rows = keep.tile([P, N], U8, name="scale_rows", align_bytes=ALIGN)
+        nc.vector.tensor_copy(scale_rows[:], scale_pool[:].indirect(offsets[:]))
         for quad in range(P // QUAD):
             src = SCALE_FROM + quad * PACK
             nc.sync.dma_start(
-                out=k_scale[QUAD * quad : QUAD * quad + PACK, :N].bitcast(I32),
+                out=k_scale[QUAD * quad : QUAD * quad + PACK, :].bitcast(I32),
                 in_=scale_rows[src : src + PACK, :].bitcast(I32),
             )
-        late = rows.tile([P, 4, N], F32, name="late", align_bytes=64, offset=0)
-        rt_sb = [late[:, 0, :], late[:, 1, :]]
-        wt_sb = [late[:, 2, :], late[:, 3, :]]
+
+        late = shared.tile([P, 2 * QT, N], F32, name="late", align_bytes=ALIGN, offset=LATE_AT)
+        rt_sb = [late[:, t, :] for t in range(QT)]
+        wt_sb = [late[:, QT + t, :] for t in range(QT)]
         for t in range(QT):
             nc.sync.dma_start(out=rt_sb[t], in_=rt[0, t * P : (t + 1) * P, :])
         for t in range(QT):
             nc.sync.dma_start(out=wt_sb[t], in_=wt[0, t * P : (t + 1) * P, :])
-        listed = [offsets[:, h * HALF // 16 : (h + 1) * HALF // 16] for h in range(2)]
-        kb_listed = rows.tile([P, N], F32, name="kb_listed", align_bytes=64, offset=10240)
-        kb_row = [kb_listed[:, :HALF], kb_listed[:, HALF:]]
+
+        halves = (slice(0, HALF), slice(HALF, N))
+        listed = [offsets[:, cols.start // LIST_GROUP : cols.stop // LIST_GROUP] for cols in halves]
+        kb_listed = shared.tile([P, N], F32, name="kb_listed", align_bytes=ALIGN, offset=KB_LISTED_AT)
         for h in (1, 0):
-            nc.scalar.activation(kb_row[h], kb_pool[:].indirect(listed[h]), COPY)
+            nc.scalar.activation(kb_listed[:, halves[h]], kb_pool[:].indirect(listed[h]), COPY)
 
         q_bf = [
-            rows.tile([P, P, PACK], BF16, name="q_bf0", align_bytes=64, offset=13248),
-            keep.tile([P, P, PACK], BF16, name="q_bf1", align_bytes=64),
+            shared.tile([P, P, PACK], BF16, name="q_bf0", align_bytes=ALIGN, offset=Q_BF0_AT),
+            keep.tile([P, P, PACK], BF16, name="q_bf1", align_bytes=ALIGN),
         ]
         for t in (1, 0):
             nc.vector.tensor_copy(
@@ -106,34 +118,35 @@ def tile_attend_link_resid_topk_kernel(tc, qT, k_words, k_scales, kb, rt, ub, wt
 
         kb_and_ub = psum.tile([P, HALF + P], F32, name="kb_and_ub")
         ub_turned = kb_and_ub[:, HALF:]
-        nc.tensor.transpose(ub_turned, ub_rows[:], ident)
+        nc.tensor.transpose(ub_turned, ub_rows[:], ident[:])
         kb_second = psum.tile([P, HALF], F32, name="kb_second")
         kb_all = [kb_and_ub[:, :HALF], kb_second[:]]
-        turned = [psum.tile([P, CH // 2, P], F32, name=f"turned{h}") for h in range(2)]
+        turned = [psum.tile([P, CHUNKS, P], F32, name=f"turned{h}") for h in range(2)]
         for h in (1, 0):
-            for c in range(CH // 2):
-                nc.tensor.transpose(turned[h][:, c, :], kb_row[h][:, c * P : (c + 1) * P], ident)
+            for c in range(CHUNKS):
+                lo = h * HALF + c * P
+                nc.tensor.transpose(turned[h][:, c, :], kb_listed[:, lo : lo + P], ident[:])
 
-        q_code = [window.tile([P, P], U32, name=f"q_code{t}", align_bytes=64, offset=4 * P * t) for t in range(QT)]
-        q_scale = [keep.tile([P, P], U8, name=f"q_scale{t}", align_bytes=64) for t in range(QT)]
+        q_code = [keep.tile([P, P], U32, name=f"q_code{t}", align_bytes=ALIGN) for t in range(QT)]
+        q_scale = [keep.tile([P, P], U8, name=f"q_scale{t}", align_bytes=ALIGN) for t in range(QT)]
         for t in (1, 0):
             nc.vector.quantize_mx(
                 out=q_code[t][:].bitcast(FP8X4), scales=q_scale[t][:], in_=q_bf[t][:].rearrange("p m j -> p (m j)")
             )
 
-        kb_col = [keep.tile([P, CH // 2], F32, name=f"kb_col{h}") for h in range(2)]
+        kb_col = [keep.tile([P, CHUNKS], F32, name=f"kb_col{h}") for h in range(2)]
         for h in (1, 0):
             nc.scalar.copy(out=kb_col[h][:], in_=turned[h][:, :, KB_ROW])
         for h in (1, 0):
-            for c in range(CH // 2):
+            for c in range(CHUNKS):
                 nc.tensor.transpose(
-                    kb_all[h][:, c * P : (c + 1) * P], kb_col[h][:, c : c + 1].to_broadcast([P, P]), ident
+                    kb_all[h][:, c * P : (c + 1) * P], kb_col[h][:, c : c + 1].to_broadcast([P, P]), ident[:]
                 )
 
         kb_sb = keep.tile([P, HALF], F32, name="kb_sb")
         nc.scalar.copy(out=kb_sb[:], in_=kb_all[1])
 
-        k_code = rows.tile([P, N], U32, name="k_code", align_bytes=64, offset=11264)
+        k_code = shared.tile([P, N], U32, name="k_code", align_bytes=ALIGN, offset=K_CODE_AT)
         acc = [
             [psum.tile([P, HALF], F32, name="acc0_0", tag="turned0"), psum.tile([P, HALF], F32, name="acc0_1")],
             [psum.tile([P, HALF], F32, name="acc1_0"), psum.tile([P, HALF], F32, name="acc1_1")],
@@ -151,16 +164,15 @@ def tile_attend_link_resid_topk_kernel(tc, qT, k_words, k_scales, kb, rt, ub, wt
             )
 
         def gather_words(h):
-            nc.vector.tensor_copy(k_code[:, h * HALF : (h + 1) * HALF], word_pool[:].bitcast(U32).indirect(listed[h]))
+            nc.vector.tensor_copy(k_code[:, halves[h]], word_pool[:].bitcast(U32).indirect(listed[h]))
 
         def score(t, h):
-            cols = slice(h * HALF, (h + 1) * HALF)
-            product(acc[t][h][:], q_code[t][:], q_scale[t][:], k_code[:, cols], k_scale[:, cols])
+            product(acc[t][h][:], q_code[t][:], q_scale[t][:], k_code[:, halves[h]], k_scale[:, halves[h]])
 
         gather_words(0)
         score(0, 0)
-        by_slot = [keep.tile([P, P], F32, name=f"by_slot{c}") for c in range(CH // 2)]
-        for c in range(CH // 2):
+        by_slot = [keep.tile([P, P], F32, name=f"by_slot{c}") for c in range(CHUNKS)]
+        for c in range(CHUNKS):
             slots = slice(c * P, (c + 1) * P)
             acc_slot = psum.tile([P, P], F32, name=f"acc_slot{c}", tag=("turned1", "acc_slot1")[c])
             product(acc_slot[:], k_code[:, slots], k_scale[:, slots], q_code[1][:], q_scale[1][:])
@@ -168,13 +180,12 @@ def tile_attend_link_resid_topk_kernel(tc, qT, k_words, k_scales, kb, rt, ub, wt
         gather_words(1)
         score(1, 1)
         score(0, 1)
-        for c in range(CH // 2):
-            nc.tensor.transpose(acc[1][0][:, c * P : (c + 1) * P], by_slot[c][:], ident)
+        for c in range(CHUNKS):
+            nc.tensor.transpose(acc[1][0][:, c * P : (c + 1) * P], by_slot[c][:], ident[:])
 
         unbiased = [keep.tile([P, N], F32, name=f"unbiased{t}") for t in range(QT)]
         resid = [keep.tile([P, N], F32, name=f"resid{t}") for t in range(QT)]
         res = [keep.tile([P, N], F32, name=f"res{t}") for t in range(QT)]
-        halves = (slice(0, HALF), slice(HALF, N))
 
         def less_kb(t, h):
             cols = halves[h]
@@ -187,7 +198,7 @@ def tile_attend_link_resid_topk_kernel(tc, qT, k_words, k_scales, kb, rt, ub, wt
         def store(t, h):
             nc.sync.dma_start(out=out[0, t * P : (t + 1) * P, halves[h]], in_=res[t][:, halves[h]])
 
-        def weigh(t, h):
+        def less_ub_and_weigh(t, h):
             cols = halves[h]
             nc.vector.scalar_tensor_tensor(
                 out=res[t][:, cols],
@@ -204,13 +215,18 @@ def tile_attend_link_resid_topk_kernel(tc, qT, k_words, k_scales, kb, rt, ub, wt
         less_kb(0, 0)
         less_kb(1, 1)
         nc.vector.scalar_tensor_tensor(
-            out=resid[0][:, first], in0=unbiased[0][:, first], scalar=ub_turned[:, UB_ROW : UB_ROW + 1], in1=acc[0][0][:], op0=SUB, op1=SUB
+            out=resid[0][:, first],
+            in0=unbiased[0][:, first],
+            scalar=ub_turned[:, UB_ROW : UB_ROW + 1],
+            in1=acc[0][0][:],
+            op0=SUB,
+            op1=SUB,
         )
         nc.gpsimd.tensor_tensor(out=res[0][:, first], in0=resid[0][:, first], in1=wt_sb[0][:, first], op=MULT)
         store(0, 0)
         less_scores(1, 1)
         less_scores(0, 1)
         nc.vector.tensor_tensor(out=resid[1][:, first], in0=rt_sb[1][:, first], in1=acc[1][0][:], op=SUB)
-        weigh(0, 1)
-        weigh(1, 1)
-        weigh(1, 0)
+        less_ub_and_weigh(0, 1)
+        less_ub_and_weigh(1, 1)
+        less_ub_and_weigh(1, 0)

@@ -12,7 +12,6 @@ U8 = mybir.dt.uint8
 FP8X4 = mybir.dt.float8_e4m3fn_x4
 SUB = mybir.AluOpType.subtract
 MULT = mybir.AluOpType.mult
-IDENTITY = mybir.ActivationFunctionType.Identity
 COPY = mybir.ActivationFunctionType.Copy
 
 P = 128
@@ -34,7 +33,7 @@ SCALE_ROWS = D // 32
 SCALE_FROM = P // 2 - SCALE_ROWS
 
 LATE_AT = 0
-SCALE_POOL_AT = LATE_AT + 4 * 2 * QT * N - ALIGN
+SCALE_POOL_AT = LATE_AT + 4 * (2 * QT - 1) * N - ALIGN
 KB_LISTED_AT = SCALE_POOL_AT + T + ALIGN
 K_CODE_AT = KB_LISTED_AT + 4 * HALF
 Q_BF0_AT = K_CODE_AT + 4 * N - ALIGN
@@ -64,6 +63,9 @@ def tile_attend_link_resid_topk_kernel(tc, qT, k_words, k_scales, kb, rt, ub, wt
         word_pool = keep.tile([P, T], I32, name="word_pool", align_bytes=ALIGN)
         nc.sync.dma_start(out=word_pool[:], in_=k_words[0].rearrange("p n r -> p (n r)").bitcast(I32))
 
+        rt_first = keep.tile([P, N], F32, name="rt_first")
+        nc.sync.dma_start(out=rt_first[:], in_=rt[0, 0:P, :])
+
         nc.gpsimd.memset(kb_pool[0:KB_ROW, :].bitcast(I32), 0)
 
         zero_col = keep.tile([P, 1], F32, name="zero_col")
@@ -92,11 +94,10 @@ def tile_attend_link_resid_topk_kernel(tc, qT, k_words, k_scales, kb, rt, ub, wt
                 in_=scale_rows[src : src + PACK, :].bitcast(I32),
             )
 
-        late = shared.tile([P, 2 * QT, N], F32, name="late", align_bytes=ALIGN, offset=LATE_AT)
-        rt_sb = [late[:, t, :] for t in range(QT)]
-        wt_sb = [late[:, QT + t, :] for t in range(QT)]
-        for t in range(QT):
-            nc.sync.dma_start(out=rt_sb[t], in_=rt[0, t * P : (t + 1) * P, :])
+        late = shared.tile([P, 2 * QT - 1, N], F32, name="late", align_bytes=ALIGN, offset=LATE_AT)
+        rt_sb = [rt_first[:], late[:, 0, :]]
+        wt_sb = [late[:, 1 + t, :] for t in range(QT)]
+        nc.sync.dma_start(out=rt_sb[1], in_=rt[0, P : 2 * P, :])
         for t in range(QT):
             nc.sync.dma_start(out=wt_sb[t], in_=wt[0, t * P : (t + 1) * P, :])
 
@@ -149,84 +150,54 @@ def tile_attend_link_resid_topk_kernel(tc, qT, k_words, k_scales, kb, rt, ub, wt
         k_code = shared.tile([P, N], U32, name="k_code", align_bytes=ALIGN, offset=K_CODE_AT)
         acc = [
             [psum.tile([P, HALF], F32, name="acc0_0", tag="turned0"), psum.tile([P, HALF], F32, name="acc0_1")],
-            [psum.tile([P, HALF], F32, name="acc1_0"), psum.tile([P, HALF], F32, name="acc1_1")],
+            [psum.tile([P, HALF], F32, name="acc1_0", tag="turned1"), psum.tile([P, HALF], F32, name="acc1_1")],
         ]
-
-        def product(dst, left, left_scale, right, right_scale):
-            nc.tensor.matmul_mx(
-                out=dst,
-                lhsT=left.bitcast(FP8X4),
-                lhsT_scale=left_scale,
-                rhs=right.bitcast(FP8X4),
-                rhs_scale=right_scale,
-                start=True,
-                stop=True,
-            )
-
-        def gather_words(h):
+        for h in range(2):
             nc.vector.tensor_copy(k_code[:, halves[h]], word_pool[:].bitcast(U32).indirect(listed[h]))
-
-        def score(t, h):
-            product(acc[t][h][:], q_code[t][:], q_scale[t][:], k_code[:, halves[h]], k_scale[:, halves[h]])
-
-        gather_words(0)
-        score(0, 0)
-        by_slot = [keep.tile([P, P], F32, name=f"by_slot{c}") for c in range(CHUNKS)]
-        for c in range(CHUNKS):
-            slots = slice(c * P, (c + 1) * P)
-            acc_slot = psum.tile([P, P], F32, name=f"acc_slot{c}", tag=("turned1", "acc_slot1")[c])
-            product(acc_slot[:], k_code[:, slots], k_scale[:, slots], q_code[1][:], q_scale[1][:])
-            nc.scalar.activation(out=by_slot[c][:], in_=acc_slot[:], func=IDENTITY, bias=kb_col[0][:, c : c + 1])
-        gather_words(1)
-        score(1, 1)
-        score(0, 1)
-        for c in range(CHUNKS):
-            nc.tensor.transpose(acc[1][0][:, c * P : (c + 1) * P], by_slot[c][:], ident[:])
+            for t in range(QT):
+                nc.tensor.matmul_mx(
+                    out=acc[t][h][:],
+                    lhsT=q_code[t][:].bitcast(FP8X4),
+                    lhsT_scale=q_scale[t][:],
+                    rhs=k_code[:, halves[h]].bitcast(FP8X4),
+                    rhs_scale=k_scale[:, halves[h]],
+                    start=True,
+                    stop=True,
+                )
 
         unbiased = [keep.tile([P, N], F32, name=f"unbiased{t}") for t in range(QT)]
         resid = [keep.tile([P, N], F32, name=f"resid{t}") for t in range(QT)]
         res = [keep.tile([P, N], F32, name=f"res{t}") for t in range(QT)]
 
-        def less_kb(t, h):
+        def less_kb(engine, t, h, spread):
             cols = halves[h]
-            nc.vector.tensor_tensor(out=unbiased[t][:, cols], in0=rt_sb[t][:, cols], in1=kb_all[h], op=SUB)
+            engine.tensor_tensor(out=unbiased[t][:, cols], in0=rt_sb[t][:, cols], in1=spread, op=SUB)
 
-        def less_scores(t, h):
-            cols = halves[h]
-            nc.vector.tensor_tensor(out=resid[t][:, cols], in0=unbiased[t][:, cols], in1=acc[t][h][:], op=SUB)
-
-        def store(t, h):
-            nc.sync.dma_start(out=out[0, t * P : (t + 1) * P, halves[h]], in_=res[t][:, halves[h]])
-
-        def less_ub_and_weigh(t, h):
+        def less_ub_and_scores(t, h):
             cols = halves[h]
             nc.vector.scalar_tensor_tensor(
-                out=res[t][:, cols],
-                in0=resid[t][:, cols],
+                out=resid[t][:, cols],
+                in0=unbiased[t][:, cols],
                 scalar=ub_turned[:, UB_ROW + t : UB_ROW + t + 1],
-                in1=wt_sb[t][:, cols],
+                in1=acc[t][h][:],
                 op0=SUB,
-                op1=MULT,
+                op1=SUB,
             )
-            store(t, h)
 
-        first, second = halves
-        nc.gpsimd.tensor_tensor(out=unbiased[0][:, second], in0=rt_sb[0][:, second], in1=kb_sb[:], op=SUB)
-        less_kb(0, 0)
-        less_kb(1, 1)
-        nc.vector.scalar_tensor_tensor(
-            out=resid[0][:, first],
-            in0=unbiased[0][:, first],
-            scalar=ub_turned[:, UB_ROW : UB_ROW + 1],
-            in1=acc[0][0][:],
-            op0=SUB,
-            op1=SUB,
-        )
-        nc.gpsimd.tensor_tensor(out=res[0][:, first], in0=resid[0][:, first], in1=wt_sb[0][:, first], op=MULT)
-        store(0, 0)
-        less_scores(1, 1)
-        less_scores(0, 1)
-        nc.vector.tensor_tensor(out=resid[1][:, first], in0=rt_sb[1][:, first], in1=acc[1][0][:], op=SUB)
-        less_ub_and_weigh(0, 1)
-        less_ub_and_weigh(1, 1)
-        less_ub_and_weigh(1, 0)
+        def weigh_and_store(engine, t, h):
+            cols = halves[h]
+            engine.tensor_tensor(out=res[t][:, cols], in0=resid[t][:, cols], in1=wt_sb[t][:, cols], op=MULT)
+            nc.sync.dma_start(out=out[0, t * P : (t + 1) * P, cols], in_=res[t][:, cols])
+
+        for t in range(QT):
+            less_kb(nc.gpsimd, t, 1, kb_sb[:])
+        for t in range(QT):
+            less_kb(nc.vector, t, 0, kb_all[0])
+        for t in range(QT):
+            less_ub_and_scores(t, 0)
+        weigh_and_store(nc.gpsimd, 0, 0)
+        for t in range(QT):
+            less_ub_and_scores(t, 1)
+        weigh_and_store(nc.vector, 0, 1)
+        for h in range(2):
+            weigh_and_store(nc.vector, 1, h)

@@ -32,6 +32,8 @@ UB_ROW = P - QT
 SCALE_ROWS = D // 32
 SCALE_FROM = P // 2 - SCALE_ROWS
 
+KB_SPLIT = 1664
+
 LATE_AT = 0
 SCALE_POOL_AT = LATE_AT + 4 * (2 * QT - 1) * N - ALIGN
 KB_LISTED_AT = SCALE_POOL_AT + T + ALIGN
@@ -55,7 +57,7 @@ def tile_attend_link_resid_topk_kernel(tc, qT, k_words, k_scales, kb, rt, ub, wt
         scale_words = scale_pool[:].bitcast(I32)
         nc.scalar.dma_start(out=scale_words[SCALE_FROM : SCALE_FROM + SCALE_ROWS, :], in_=k_scales[0].bitcast(I32))
         kb_pool = keep.tile([P, T], F32, name="kb_pool", align_bytes=ALIGN)
-        nc.scalar.dma_start(out=kb_pool[KB_ROW:P, :], in_=kb[0:1, :])
+        nc.sync.dma_start(out=kb_pool[KB_ROW:P, :], in_=kb[0:1, :])
         q_raw = keep.tile([P, PACK, NQ], F32, name="q_raw", align_bytes=ALIGN)
         nc.sync.dma_start(out=q_raw[:], in_=qT[0].rearrange("(p j) w -> p j w", j=PACK))
         ub_rows = keep.tile([P, P], F32, name="ub_rows")
@@ -66,11 +68,11 @@ def tile_attend_link_resid_topk_kernel(tc, qT, k_words, k_scales, kb, rt, ub, wt
         rt_first = keep.tile([P, N], F32, name="rt_first")
         nc.sync.dma_start(out=rt_first[:], in_=rt[0, 0:P, :])
 
-        nc.gpsimd.memset(kb_pool[0:KB_ROW, :].bitcast(I32), 0)
-
         zero_col = keep.tile([P, 1], F32, name="zero_col")
-        nc.vector.memset(zero_col[:], 0.0)
+        nc.gpsimd.memset(zero_col[:], 0.0)
         nc.scalar.copy(out=ub_rows[0:UB_ROW, :], in_=zero_col[0:UB_ROW, :].to_broadcast([UB_ROW, P]))
+        kb_words = kb_pool[0:KB_ROW, :].bitcast(I32)
+        nc.gpsimd.memset(kb_words[:, :KB_SPLIT], 0)
 
         def zero_beside_gpsimd(words):
             last = words.shape[1] - 1
@@ -79,9 +81,9 @@ def tile_attend_link_resid_topk_kernel(tc, qT, k_words, k_scales, kb, rt, ub, wt
 
         zero_beside_gpsimd(scale_words[0:SCALE_FROM, :])
         zero_beside_gpsimd(scale_words[SCALE_FROM + SCALE_ROWS :, :])
+        zero_beside_gpsimd(kb_words[:, KB_SPLIT:])
         ident = keep.tile([P, P], F32, name="ident")
-        zero_beside_gpsimd(ident[:])
-        make_identity(nc, ident[:], nomemset=True)
+        make_identity(nc, ident[:])
 
         k_scale = keep.tile([P, N], U8, name="k_scale", align_bytes=ALIGN)
         zero_beside_gpsimd(k_scale[:].bitcast(I32))
@@ -119,7 +121,6 @@ def tile_attend_link_resid_topk_kernel(tc, qT, k_words, k_scales, kb, rt, ub, wt
 
         kb_and_ub = psum.tile([P, HALF + P], F32, name="kb_and_ub")
         ub_turned = kb_and_ub[:, HALF:]
-        nc.tensor.transpose(ub_turned, ub_rows[:], ident[:])
         kb_second = psum.tile([P, HALF], F32, name="kb_second")
         kb_all = [kb_and_ub[:, :HALF], kb_second[:]]
         turned = [psum.tile([P, CHUNKS, P], F32, name=f"turned{h}") for h in range(2)]
@@ -127,6 +128,8 @@ def tile_attend_link_resid_topk_kernel(tc, qT, k_words, k_scales, kb, rt, ub, wt
             for c in range(CHUNKS):
                 lo = h * HALF + c * P
                 nc.tensor.transpose(turned[h][:, c, :], kb_listed[:, lo : lo + P], ident[:])
+
+        nc.tensor.transpose(ub_turned, ub_rows[:], ident[:])
 
         q_code = [keep.tile([P, P], U32, name=f"q_code{t}", align_bytes=ALIGN) for t in range(QT)]
         q_scale = [keep.tile([P, P], U8, name=f"q_scale{t}", align_bytes=ALIGN) for t in range(QT)]

@@ -100,10 +100,11 @@ def tile_attend_link_resid_topk_kernel(tc, qT, k_words, k_scales, kb, rt, ub, wt
         rt_sb = [rt_first[:], late[:, 0, :]]
         wt_sb = [late[:, 1 + t, :] for t in range(QT)]
         nc.sync.dma_start(out=rt_sb[1], in_=rt[0, P : 2 * P, :])
-        for t in range(QT):
-            nc.sync.dma_start(out=wt_sb[t], in_=wt[0, t * P : (t + 1) * P, :])
-
+        nc.sync.dma_start(out=wt_sb[0], in_=wt[0, 0:P, :])
         halves = (slice(0, HALF), slice(HALF, N))
+        for cols in halves:
+            nc.sync.dma_start(out=wt_sb[1][:, cols], in_=wt[0, P : 2 * P, cols])
+
         listed = [offsets[:, cols.start // LIST_GROUP : cols.stop // LIST_GROUP] for cols in halves]
         kb_listed = shared.tile([P, N], F32, name="kb_listed", align_bytes=ALIGN, offset=KB_LISTED_AT)
         for h in (1, 0):

@@ -34,6 +34,8 @@ SCALE_FROM = P // 2 - SCALE_ROWS
 
 KB_SPLIT = 1664
 
+GPSIMD_COLS = 192
+
 LATE_AT = 0
 SCALE_POOL_AT = LATE_AT + 4 * (2 * QT - 1) * N - ALIGN
 KB_LISTED_AT = SCALE_POOL_AT + T + ALIGN
@@ -188,8 +190,7 @@ def tile_attend_link_resid_topk_kernel(tc, qT, k_words, k_scales, kb, rt, ub, wt
                 op1=SUB,
             )
 
-        def weigh_and_store(engine, t, h):
-            cols = halves[h]
+        def weigh_and_store(engine, t, cols):
             engine.tensor_tensor(out=res[t][:, cols], in0=resid[t][:, cols], in1=wt_sb[t][:, cols], op=MULT)
             nc.sync.dma_start(out=out[0, t * P : (t + 1) * P, cols], in_=res[t][:, cols])
 
@@ -199,9 +200,9 @@ def tile_attend_link_resid_topk_kernel(tc, qT, k_words, k_scales, kb, rt, ub, wt
             less_kb(nc.vector, t, 0, kb_all[0])
         for t in range(QT):
             less_ub_and_scores(t, 0)
-        weigh_and_store(nc.gpsimd, 0, 0)
+        weigh_and_store(nc.gpsimd, 0, slice(0, GPSIMD_COLS))
         for t in range(QT):
             less_ub_and_scores(t, 1)
-        weigh_and_store(nc.vector, 0, 1)
-        for h in range(2):
-            weigh_and_store(nc.vector, 1, h)
+        weigh_and_store(nc.vector, 1, halves[0])
+        weigh_and_store(nc.vector, 0, slice(GPSIMD_COLS, N))
+        weigh_and_store(nc.vector, 1, halves[1])

from contextlib import ExitStack

import concourse.mybir as mybir
from concourse.masks import make_identity

F32 = mybir.dt.float32
BF16 = mybir.dt.bfloat16
I32 = mybir.dt.int32
U32 = mybir.dt.uint32
U16 = mybir.dt.uint16
U8 = mybir.dt.uint8
FP8X4 = mybir.dt.float8_e4m3fn_x4
SUB = mybir.AluOpType.subtract
MULT = mybir.AluOpType.mult
COPY = mybir.ActivationFunctionType.Copy

P = 128
PACK = 4
D = 512
NQ = 256
N = 512
T = 2048
QT = NQ // P
QUAD = 32
HALF = N // 2
CHUNKS = HALF // P
LIST_GROUP = 16
ALIGN = 64

KB_ROW = P - 1
UB_ROW = P - QT
SCALE_ROWS = D // 32
SCALE_FROM = P // 2 - SCALE_ROWS

KB_SPLIT = 1664

GPSIMD_COLS = 192

LATE_AT = 0
SCALE_POOL_AT = LATE_AT + 4 * (2 * QT - 1) * N - ALIGN
KB_LISTED_AT = SCALE_POOL_AT + T + ALIGN
K_CODE_AT = KB_LISTED_AT + 4 * HALF
Q_BF0_AT = K_CODE_AT + 4 * N - ALIGN

FLOPS = 2 * D * NQ * N
BYTES = 4 * D * NQ + D * T + SCALE_ROWS * T + 4 * T + 3 * 4 * NQ * N + 4 * NQ + 2 * P * (N // LIST_GROUP)


def tile_attend_link_resid_topk_kernel(tc, qT, k_words, k_scales, kb, rt, ub, wt, offs, out):
    nc = tc.nc
    with ExitStack() as ctx:
        keep = ctx.enter_context(tc.tile_pool(name="keep", bufs=1))
        shared = ctx.enter_context(tc.tile_pool(name="shared", bufs=1))
        psum = ctx.enter_context(tc.psum_pool(name="psum", bufs=1))

        offsets = keep.tile([P, N // LIST_GROUP], U16, name="offsets")
        nc.sync.dma_start(offsets[:], offs)
        scale_pool = shared.tile([P, T], U8, name="scale_pool", align_bytes=ALIGN, offset=SCALE_POOL_AT)
        scale_words = scale_pool[:].bitcast(I32)
        nc.scalar.dma_start(out=scale_words[SCALE_FROM : SCALE_FROM + SCALE_ROWS, :], in_=k_scales[0].bitcast(I32))
        kb_pool = keep.tile([P, T], F32, name="kb_pool", align_bytes=ALIGN)
        nc.sync.dma_start(out=kb_pool[KB_ROW:P, :], in_=kb[0:1, :])
        q_raw = keep.tile([P, PACK, NQ], F32, name="q_raw", align_bytes=ALIGN)
        nc.sync.dma_start(out=q_raw[:], in_=qT[0].rearrange("(p j) w -> p j w", j=PACK))
        ub_rows = keep.tile([P, P], F32, name="ub_rows")
        nc.sync.dma_start(out=ub_rows[UB_ROW:P, :], in_=ub[0].rearrange("(t p) o -> t (p o)", t=QT))
        word_pool = keep.tile([P, T], I32, name="word_pool", align_bytes=ALIGN)
        nc.sync.dma_start(out=word_pool[:], in_=k_words[0].rearrange("p n r -> p (n r)").bitcast(I32))

        rt_first = keep.tile([P, N], F32, name="rt_first")
        nc.sync.dma_start(out=rt_first[:], in_=rt[0, 0:P, :])

        zero_col = keep.tile([P, 1], F32, name="zero_col")
        nc.gpsimd.memset(zero_col[:], 0.0)
        nc.scalar.copy(out=ub_rows[0:UB_ROW, :], in_=zero_col[0:UB_ROW, :].to_broadcast([UB_ROW, P]))
        kb_words = kb_pool[0:KB_ROW, :].bitcast(I32)
        nc.gpsimd.memset(kb_words[:, :KB_SPLIT], 0)

        def zero_beside_gpsimd(words):
            last = words.shape[1] - 1
            nc.vector.memset(words[:, :last], 0)
            nc.vector.memset(words[:, last:], 0)

        zero_beside_gpsimd(scale_words[0:SCALE_FROM, :])
        zero_beside_gpsimd(scale_words[SCALE_FROM + SCALE_ROWS :, :])
        zero_beside_gpsimd(kb_words[:, KB_SPLIT:])
        ident = keep.tile([P, P], F32, name="ident")
        make_identity(nc, ident[:])

        k_scale = keep.tile([P, N], U8, name="k_scale", align_bytes=ALIGN)
        zero_beside_gpsimd(k_scale[:].bitcast(I32))
        scale_rows = keep.tile([P, N], U8, name="scale_rows", align_bytes=ALIGN)
        nc.vector.tensor_copy(scale_rows[:], scale_pool[:].indirect(offsets[:]))
        for quad in range(P // QUAD):
            src = SCALE_FROM + quad * PACK
            nc.sync.dma_start(
                out=k_scale[QUAD * quad : QUAD * quad + PACK, :].bitcast(I32),
                in_=scale_rows[src : src + PACK, :].bitcast(I32),
            )

        late = shared.tile([P, 2 * QT - 1, N], F32, name="late", align_bytes=ALIGN, offset=LATE_AT)
        rt_sb = [rt_first[:], late[:, 0, :]]
        wt_sb = [late[:, 1 + t, :] for t in range(QT)]
        nc.sync.dma_start(out=rt_sb[1], in_=rt[0, P : 2 * P, :])
        nc.sync.dma_start(out=wt_sb[0], in_=wt[0, 0:P, :])
        halves = (slice(0, HALF), slice(HALF, N))
        for cols in halves:
            nc.sync.dma_start(out=wt_sb[1][:, cols], in_=wt[0, P : 2 * P, cols])

        listed = [offsets[:, cols.start // LIST_GROUP : cols.stop // LIST_GROUP] for cols in halves]
        kb_listed = shared.tile([P, N], F32, name="kb_listed", align_bytes=ALIGN, offset=KB_LISTED_AT)
        for h in (1, 0):
            nc.scalar.activation(kb_listed[:, halves[h]], kb_pool[:].indirect(listed[h]), COPY)

        q_bf = [
            shared.tile([P, P, PACK], BF16, name="q_bf0", align_bytes=ALIGN, offset=Q_BF0_AT),
            keep.tile([P, P, PACK], BF16, name="q_bf1", align_bytes=ALIGN),
        ]
        for t in (1, 0):
            nc.vector.tensor_copy(
                q_bf[t][:].rearrange("p (c i) j -> p c j i", i=PACK),
                q_raw[:, :, t * P : (t + 1) * P].rearrange("p j (c i) -> p c j i", i=PACK),
            )

        kb_and_ub = psum.tile([P, HALF + P], F32, name="kb_and_ub")
        ub_turned = kb_and_ub[:, HALF:]
        kb_second = psum.tile([P, HALF], F32, name="kb_second")
        kb_all = [kb_and_ub[:, :HALF], kb_second[:]]
        turned = [psum.tile([P, CHUNKS, P], F32, name=f"turned{h}") for h in range(2)]
        for h in (1, 0):
            for c in range(CHUNKS):
                lo = h * HALF + c * P
                nc.tensor.transpose(turned[h][:, c, :], kb_listed[:, lo : lo + P], ident[:])

        nc.tensor.transpose(ub_turned, ub_rows[:], ident[:])

        q_code = [keep.tile([P, P], U32, name=f"q_code{t}", align_bytes=ALIGN) for t in range(QT)]
        q_scale = [keep.tile([P, P], U8, name=f"q_scale{t}", align_bytes=ALIGN) for t in range(QT)]
        for t in (1, 0):
            nc.vector.quantize_mx(
                out=q_code[t][:].bitcast(FP8X4), scales=q_scale[t][:], in_=q_bf[t][:].rearrange("p m j -> p (m j)")
            )

        kb_col = [keep.tile([P, CHUNKS], F32, name=f"kb_col{h}") for h in range(2)]
        for h in (1, 0):
            nc.scalar.copy(out=kb_col[h][:], in_=turned[h][:, :, KB_ROW])
        for h in (1, 0):
            for c in range(CHUNKS):
                nc.tensor.transpose(
                    kb_all[h][:, c * P : (c + 1) * P], kb_col[h][:, c : c + 1].to_broadcast([P, P]), ident[:]
                )

        kb_sb = keep.tile([P, HALF], F32, name="kb_sb")
        nc.scalar.copy(out=kb_sb[:], in_=kb_all[1])

        k_code = shared.tile([P, N], U32, name="k_code", align_bytes=ALIGN, offset=K_CODE_AT)
        acc = [
            [psum.tile([P, HALF], F32, name="acc0_0", tag="turned0"), psum.tile([P, HALF], F32, name="acc0_1")],
            [psum.tile([P, HALF], F32, name="acc1_0", tag="turned1"), psum.tile([P, HALF], F32, name="acc1_1")],
        ]
        for h in range(2):
            nc.vector.tensor_copy(k_code[:, halves[h]], word_pool[:].bitcast(U32).indirect(listed[h]))
            for t in range(QT):
                nc.tensor.matmul_mx(
                    out=acc[t][h][:],
                    lhsT=q_code[t][:].bitcast(FP8X4),
                    lhsT_scale=q_scale[t][:],
                    rhs=k_code[:, halves[h]].bitcast(FP8X4),
                    rhs_scale=k_scale[:, halves[h]],
                    start=True,
                    stop=True,
                )

        unbiased = [keep.tile([P, N], F32, name=f"unbiased{t}") for t in range(QT)]
        resid = [keep.tile([P, N], F32, name=f"resid{t}") for t in range(QT)]
        res = [keep.tile([P, N], F32, name=f"res{t}") for t in range(QT)]

        def less_kb(engine, t, h, spread):
            cols = halves[h]
            engine.tensor_tensor(out=unbiased[t][:, cols], in0=rt_sb[t][:, cols], in1=spread, op=SUB)

        def less_ub_and_scores(t, h):
            cols = halves[h]
            nc.vector.scalar_tensor_tensor(
                out=resid[t][:, cols],
                in0=unbiased[t][:, cols],
                scalar=ub_turned[:, UB_ROW + t : UB_ROW + t + 1],
                in1=acc[t][h][:],
                op0=SUB,
                op1=SUB,
            )

        def weigh_and_store(engine, t, cols):
            engine.tensor_tensor(out=res[t][:, cols], in0=resid[t][:, cols], in1=wt_sb[t][:, cols], op=MULT)
            nc.sync.dma_start(out=out[0, t * P : (t + 1) * P, cols], in_=res[t][:, cols])

        for t in range(QT):
            less_kb(nc.gpsimd, t, 1, kb_sb[:])
        for t in range(QT):
            less_kb(nc.vector, t, 0, kb_all[0])
        for t in range(QT):
            less_ub_and_scores(t, 0)
        weigh_and_store(nc.gpsimd, 0, slice(0, GPSIMD_COLS))
        for t in range(QT):
            less_ub_and_scores(t, 1)
        weigh_and_store(nc.vector, 1, halves[0])
        weigh_and_store(nc.vector, 0, slice(GPSIMD_COLS, N))
        weigh_and_store(nc.vector, 1, halves[1])
